import numpy as np
import ml_dtypes


def mxq(x, axis, fmt="e4m3"):
    dtype, down = {"e4m3": (ml_dtypes.float8_e4m3fn, 7), "e5m2": (ml_dtypes.float8_e5m2, 14)}[fmt]
    v = np.moveaxis(np.asarray(x, np.float32).astype(ml_dtypes.bfloat16).astype(np.float64), axis, -1)
    blocks = v.reshape(v.shape[:-1] + (-1, 32))
    amax = np.abs(blocks).max(-1, keepdims=True)
    byte = np.maximum(np.where(amax > 0, np.frexp(amax)[1] - 1 + 127, 0) - down, 1)
    scale = np.exp2(byte - 127.0)
    codes = (blocks / scale).astype(np.float32).astype(dtype).astype(np.float64)
    return np.moveaxis((codes * scale).reshape(v.shape), -1, axis)


WIDE = False


def mx_kscale(k):
    if not WIDE:
        return np.ones(k)
    levels = np.array([10, -10, 5, -5, 0])
    if k % 512:
        return np.exp2(np.random.permutation(np.resize(levels, k // 32))).repeat(32)
    a = np.empty((k // 512, 16))
    for p in range(k // 512):
        a[p, :8] = np.random.permutation(np.resize(levels, 8))
        for g in range(8):
            far = levels[np.abs(levels - a[p, g]) >= 10]
            a[p, g + 8] = far[np.random.randint(len(far))]
    return np.exp2(a.ravel()).repeat(32)


BF16 = ml_dtypes.bfloat16


def bf(x):
    return np.asarray(x, np.float32).astype(BF16)


def f64(x):
    return np.asarray(x).astype(np.float64)


E2M1 = np.array([0.0, 0.5, 1.0, 1.5, 2.0, 3.0, 4.0, 6.0, -0.0, -0.5, -1.0, -1.5, -2.0, -3.0, -4.0, -6.0])


def pack_weight(w, fmt):
    k, n = w.shape
    w = f64(bf(w)).reshape(k // 32, 32, n)
    amax = np.abs(w).max(1)
    if fmt == "e4m3":
        byte = np.frexp(amax)[1] - 1 + 127 - 7
    else:
        mant, ex = np.frexp(amax / 6.0)
        byte = np.where(mant > 0.5, ex, ex - 1) + 127
    byte = np.clip(np.where(amax > 0, byte, 1), 1, 254)
    scaled = (w * np.exp2(127.0 - byte)[:, None, :]).reshape(k, n).astype(np.float32)
    by_word = np.ascontiguousarray(scaled.reshape(k // 512, 128, 4, n).transpose(0, 1, 3, 2))
    if fmt == "e4m3":
        words = by_word.astype(ml_dtypes.float8_e4m3fn).view(np.uint8)
    else:
        c = by_word.astype(ml_dtypes.float4_e2m1fn).view(np.uint8) & 0xF
        words = c[..., 0::2] | (c[..., 1::2] << 4)
    return np.ascontiguousarray(words), np.ascontiguousarray(byte.astype(np.uint8).reshape(k // 512, 16, n))


def unpack_weight(words, scales, fmt):
    g, p, n, _ = words.shape
    if fmt == "e4m3":
        vals = np.ascontiguousarray(words).view(ml_dtypes.float8_e4m3fn).astype(np.float64)
    else:
        nib = np.empty((g, p, n, 4), np.uint8)
        nib[..., 0::2] = words & 0xF
        nib[..., 1::2] = words >> 4
        vals = E2M1[nib]
    vals = vals * np.repeat(np.exp2(scales.astype(np.float64) - 127.0), 8, axis=1)[..., None]
    return vals.transpose(0, 1, 3, 2).reshape(g * 512, n)
def pack4(w):
    words, scales = pack_weight(w, "e2m1")
    return words.reshape(words.shape[0], 128, -1), scales


def unpack4(words, scales):
    return unpack_weight(words.reshape(words.shape[0], 128, -1, 2), scales, "e2m1")


T, D, P, G, R = 1024, 1024, 2048, 512, 512


def setup_inputs():
    s, t, u = mx_kscale(D), mx_kscale(P), mx_kscale(T)
    a = 2.0 * np.random.standard_normal((P, D))
    a = np.exp(a - a.max(axis=1, keepdims=True))
    a = a / a.sum(axis=1, keepdims=True)
    c_words, c_scales = pack4(np.random.standard_normal((P, G)) / np.sqrt(P) / t[:, None])
    return {"y": bf(4.0 * np.random.standard_normal((T, D)) * s),
            "w": bf(a / s),
            "z": bf(0.8 * np.random.standard_normal((T, P))),
            "prec": bf(np.exp(0.3 * np.random.standard_normal((T, P))) * t * u[:, None]),
            "c_words": c_words,
            "c_scales": c_scales,
            "win": bf(np.random.standard_normal((R, T)) / np.sqrt(T) / u)}


def reference(y, w, z, prec, c_words, c_scales, win):
    synth = mxq(f64(y), 1, "e4m3") @ mxq(f64(w), 1, "e4m3").T
    v = np.square(synth - f64(z)) * f64(prec)
    by_unit = mxq(v, 1, "e4m3") @ unpack4(c_words, c_scales)
    by_time = mxq(f64(win), 1, "e4m3") @ mxq(v, 0, "e4m3")
    return by_unit, by_time

@@ -1,0 +1,330 @@
+from contextlib import ExitStack
+
+import concourse.mybir as mybir
+from concourse.masks import make_identity
+
+T, D, NP, G, R = 1024, 1024, 2048, 512, 512
+FLOPS = 2 * T * D * NP + 2 * T * NP * G + 2 * R * T * NP
+
+F32 = mybir.dt.float32
+BF16 = mybir.dt.bfloat16
+U32 = mybir.dt.uint32
+I32 = mybir.dt.int32
+U8 = mybir.dt.uint8
+FP8X4 = mybir.dt.float8_e4m3fn_x4
+FP4X4 = mybir.dt.float4_e2m1fn_x4
+ALU = mybir.AluOpType
+ACT = mybir.ActivationFunctionType
+
+P = 128
+KP = 512
+UNITS = 16
+AHEAD = 5
+SHARE_EARLY = 320
+SHARE_LATE = 192
+SHARE_LAST = 160
+
+
+def tile_synthetic_control_placebos_s8_kernel(tc, y, w, z, prec, c_words, c_scales, win, out_0, out_1):
+    nc = tc.nc
+    with ExitStack() as ctx:
+        keep = ctx.enter_context(tc.tile_pool(name="keep", bufs=1))
+        flow = ctx.enter_context(tc.tile_pool(name="flow", bufs=2))
+        synth_ps = ctx.enter_context(tc.psum_pool(name="synth_ps", bufs=4))
+        aux_ps = ctx.enter_context(tc.psum_pool(name="aux_ps", bufs=4))
+        ctx.enter_context(tc.manual_schedule())
+
+        ident = keep.tile([P, P], F32, name="ident")
+        make_identity(nc, ident[:])
+        warm = keep.tile([P, 8], F32, name="warm")
+        nc.scalar.activation(out=warm[:], in_=ident[:, 0:8], func=ACT.Square)
+        c_plane = keep.tile([P, 4 * G], U8, name="c_plane", align_bytes=64)
+        nc.gpsimd.memset(c_plane[:].bitcast(U32), 0)
+        c_codes = keep.tile([P, 4 * 2 * G], U8, name="c_codes", align_bytes=64)
+
+        rows, zt, pt, acc, dt, st, xt, astage = {}, {}, {}, {}, {}, {}, {}, {}
+        banks, stage, quant, outs = {}, {}, {}, {}
+
+        def row_source(key):
+            kind, grp, i = key
+            if kind == "w":
+                return w[KP * grp + P * i : KP * grp + P * (i + 1), :]
+            src = y if kind == "y" else win
+            return src[KP * grp : KP * (grp + 1), :].rearrange("(m j) k -> m j k", j=4)[:, i, :]
+
+        def load_rows(key):
+            rows[key] = flow.tile([P, D], BF16, name="rows", bufs=14)
+            nc.sync.dma_start(out=rows[key][:], in_=row_source(key))
+
+        def load_cells(src, store, name, n):
+            gt, pb, h = n // 8, (n // 2) % 4, n % 2
+            store[n] = flow.tile([P, 2 * KP], BF16, name=name, bufs=7)
+            view = src[KP * gt : KP * (gt + 1), KP * pb : KP * (pb + 1)].rearrange("(m j) c -> m j c", j=4)
+            nc.sync.dma_start(out=store[n][:].rearrange("p (j c) -> p j c", j=2), in_=view[:, 2 * h : 2 * h + 2, :])
+
+        def load_c():
+            nc.sync.dma_start(
+                out=c_codes[:].bitcast(I32).rearrange("p (g n) -> p g n", g=4),
+                in_=c_words.bitcast(I32).rearrange("g p n -> p g n"),
+            )
+            for q in range(4):
+                nc.sync.dma_start(
+                    out=c_plane[32 * q : 32 * q + 4, :].bitcast(I32).rearrange("r (g n) -> r g n", g=4),
+                    in_=c_scales.bitcast(I32)[:, 4 * q : 4 * q + 4, :].rearrange("g r n -> r g n"),
+                )
+
+        jobs = [("y", 0, 0), ("w", 0, 0), ("w", 0, 1), ("y", 0, 1)]
+        jobs = jobs + [("w", pb, g) for pb in range(1, 4) for g in range(2)]
+        jobs = jobs + [("y", 1, 0), ("y", 1, 1), ("win", 0, 0), ("win", 0, 1)]
+
+        def slots(job):
+            kind, grp, i = job
+            if kind == "y":
+                return [((kind, grp, 2 * i + j), g) for j in range(2) for g in range(2)]
+            return [((kind, grp, a), i) for a in range(4)]
+
+        def load_job(q):
+            for key, g in slots(jobs[q]):
+                if key not in rows:
+                    load_rows(key)
+
+        def turn_job(q, half):
+            bank = aux_ps.tile([P, KP], F32, name="aux")
+            for s, (key, g) in enumerate(slots(jobs[q])[2 * half : 2 * half + 2]):
+                words = rows[key][:].bitcast(F32)
+                for u in range(2):
+                    col = P * (2 * s + u)
+                    nc.tensor.transpose(bank[:, col : col + P], words[:, 256 * g + u : 256 * (g + 1) : 2], ident[:])
+            banks[("job", q, half)] = bank
+
+        def pair_copy(eng, dst, bank, order):
+            out = dst.bitcast(F32).rearrange("p (s m u) -> p s m u", s=2, u=2)
+            src = bank[:].rearrange(order, s=2, u=2)
+            if eng == "S":
+                nc.scalar.copy(out=out, in_=src)
+            else:
+                nc.vector.tensor_copy(out=out, in_=src)
+
+        def copy_job(q, half, eng):
+            if half == 0:
+                stage[q] = flow.tile([P, 4 * KP], BF16, name="stage", bufs=3, align_bytes=64)
+            pair_copy(eng, stage[q][:, 1024 * half : 1024 * (half + 1)], banks[("job", q, half)], "p (s u m) -> p s m u")
+
+        def quantise(key, src, width):
+            codes = keep.tile([P, width], U32, name="codes_%s_%d_%d" % key, align_bytes=64)
+            plane = keep.tile([P, width], U8, name="plane_%s_%d_%d" % key, align_bytes=64)
+            nc.vector.quantize_mx(out=codes[:].bitcast(FP8X4), scales=plane[:], in_=src)
+            quant[key] = (codes, plane)
+
+        def mx(out, left, lcol, right, start, stop):
+            nc.tensor.matmul_mx(
+                out=out,
+                lhsT=left[0][:, lcol : lcol + P].bitcast(FP8X4),
+                lhsT_scale=left[1][:, lcol : lcol + P],
+                rhs=right[0],
+                rhs_scale=right[1],
+                start=start,
+                stop=stop,
+            )
+
+        def moving(key):
+            return (quant[key][0][:].bitcast(FP8X4), quant[key][1][:])
+
+        def synth(n):
+            gt, pb, h = n // 8, (n // 2) % 4, n % 2
+            for j in range(2):
+                bank = synth_ps.tile([P, KP], F32, name="synth")
+                for g in range(2):
+                    mx(bank[:], quant[("y", gt, h)], P * (2 * j + g), moving(("w", pb, g)), g == 0, g == 1)
+                acc[(n, j)] = bank
+
+        def subtract(n):
+            dt[n] = flow.tile([P, 2 * KP], F32, name="gap", bufs=3)
+            for j in range(2):
+                cols = slice(KP * j, KP * (j + 1))
+                nc.vector.tensor_tensor(out=dt[n][:, cols], in0=acc[(n, j)][:], in1=zt[n][:, cols], op=ALU.subtract)
+
+        def square(n):
+            st[n] = flow.tile([P, 2 * KP], F32, name="sq", bufs=3)
+            nc.scalar.activation(
+                out=st[n][:].rearrange("p (u c e) -> p u c e", u=2, e=2),
+                in_=dt[n][:].rearrange("p (c u e) -> p u c e", u=2, e=2),
+                func=ACT.Square,
+            )
+
+        def weigh(n):
+            b, h = n // 2, n % 2
+            if h == 0:
+                xt[b] = flow.tile([P, 4 * KP], BF16, name="v", bufs=3)
+            nc.vector.tensor_tensor(
+                out=xt[b][:, 1024 * h : 1024 * (h + 1)].rearrange("p (u c e) -> p u c e", u=2, e=2),
+                in0=st[n][:].rearrange("p (u c e) -> p u c e", u=2, e=2),
+                in1=pt[n][:].rearrange("p (c u e) -> p u c e", u=2, e=2),
+                op=ALU.mult,
+            )
+
+        def turn_v(n):
+            b, h = n // 2, n % 2
+            bank = aux_ps.tile([P, KP], F32, name="aux")
+            words = xt[b][:].bitcast(F32)
+            for i in range(4):
+                nc.tensor.transpose(bank[:, P * i : P * (i + 1)], words[:, KP * h + P * i : KP * h + P * (i + 1)], ident[:])
+            banks[("v", n)] = bank
+
+        def copy_v(n, eng):
+            stage[("v", n)] = flow.tile([P, 2 * KP], BF16, name="vstage", bufs=3, align_bytes=64)
+            pair_copy(eng, stage[("v", n)][:], banks[("v", n)], "p (u s m) -> p s m u")
+
+        def interleave(b, eng, lo, hi):
+            if b not in astage:
+                astage[b] = flow.tile([P, 4 * KP], BF16, name="astage", bufs=2, align_bytes=64)
+            src = xt[b][:].rearrange("p (h u j c i) -> p u c h j i", h=2, u=2, j=2, i=4)
+            dst = astage[b][:].rearrange("p (u c i h j) -> p u c h j i", u=2, i=4, h=2, j=2)
+            for u in range(2):
+                c0, c1 = max(lo - 256 * u, 0) // 4, min(hi - 256 * u, 256) // 4
+                if c1 > c0:
+                    if eng == "S":
+                        nc.scalar.copy(out=dst[:, u, c0:c1], in_=src[:, u, c0:c1])
+                    else:
+                        nc.vector.tensor_copy(out=dst[:, u, c0:c1], in_=src[:, u, c0:c1])
+
+        def unit_passes(gt, j, pool, name, first, last):
+            if first == 0:
+                outs[("unit", gt, j)] = pool.tile([P, KP], F32, name=name)
+            for pb in range(first, last):
+                rhs = (c_codes[:, 2 * G * pb : 2 * G * (pb + 1)].bitcast(FP4X4), c_plane[:, G * pb : G * (pb + 1)])
+                mx(outs[("unit", gt, j)][:], quant[("vt", 8 * gt + 2 * pb + j // 2, 0)], P * (j % 2), rhs, pb == 0, pb == 3)
+
+        def time_passes(pb, a, first, last):
+            if first == 0:
+                outs[("time", pb, a)] = aux_ps.tile([P, KP], F32, name="aux")
+            for gt in range(first, last):
+                mx(outs[("time", pb, a)][:], quant[("win", 0, gt)], P * a, moving(("v", 4 * gt + pb, 0)), gt == 0, gt == 1)
+
+        def emit(key, eng):
+            kind, grp, i = key
+            res = flow.tile([P, KP], F32, name="res", bufs=8)
+            if kind == "unit":
+                out, src = res[:], outs[key][:]
+                dest = out_0[KP * grp : KP * (grp + 1), :].rearrange("(m j) n -> m j n", j=4)[:, i, :]
+            else:
+                out = res[:].rearrange("p (c u e) -> p c u e", u=2, e=2)
+                src = outs[key][:].rearrange("p (u c e) -> p c u e", u=2, e=2)
+                dest = out_1.rearrange("(m a) n -> m a n", a=4)[:, i, KP * grp : KP * (grp + 1)]
+            if eng == "S":
+                nc.scalar.copy(out=out, in_=src)
+            else:
+                nc.vector.tensor_copy(out=out, in_=src)
+            nc.sync.dma_start(out=dest, in_=res[:])
+
+        def step_outputs(n):
+            if n in (9, 10):
+                return [("unit", 0, 2 * (n - 9) + i) for i in range(2)]
+            if 11 <= n <= 16:
+                return [("time", (n - 11) // 2, 2 * ((n - 11) % 2) + i) for i in range(2)]
+            return []
+
+        for q in range(4):
+            load_job(q)
+        load_cells(z, zt, "zc", 0)
+        load_cells(prec, pt, "pc", 0)
+        load_job(4)
+        load_cells(z, zt, "zc", 1)
+        for q in range(4):
+            for half in range(2):
+                turn_job(q, half)
+                copy_job(q, half, "SV"[half])
+            if q > 0:
+                quantise(jobs[q - 1], stage[q - 1][:], KP)
+        load_cells(prec, pt, "pc", 1)
+        load_job(6)
+        for n in range(2, AHEAD):
+            load_cells(z, zt, "zc", n)
+            load_cells(prec, pt, "pc", n)
+        synth(0)
+        for half in range(2):
+            turn_job(4, half)
+            copy_job(4, half, "S")
+        quantise(jobs[3], stage[3][:], KP)
+
+        for n in range(UNITS):
+            q = n + 5
+            if n + AHEAD < UNITS:
+                load_cells(z, zt, "zc", n + AHEAD)
+                load_cells(prec, pt, "pc", n + AHEAD)
+            if q + 3 < len(jobs):
+                load_job(q + 3)
+            if n == 4:
+                load_c()
+            if n >= 2:
+                turn_v(n - 2)
+            if q < len(jobs):
+                turn_job(q, 0)
+                turn_job(q, 1)
+            subtract(n)
+            if n >= 2:
+                copy_v(n - 2, "S")
+            for key in step_outputs(n - 1)[1:]:
+                emit(key, "S")
+            if q - 1 < len(jobs):
+                quantise(jobs[q - 1], stage[q - 1][:], KP)
+            if n >= 3 and n % 2 == 1:
+                quantise(("v", (n - 3) // 2, 0), astage[(n - 3) // 2][:], KP)
+            square(n)
+            if n + 1 < UNITS:
+                synth(n + 1)
+            for kind, grp, i in step_outputs(n):
+                if kind == "unit":
+                    unit_passes(grp, i, aux_ps, "aux", 0, 4)
+                else:
+                    time_passes(grp, i, 0, 2)
+            if n + 1 == UNITS:
+                for j in range(2):
+                    unit_passes(1, j, synth_ps, "synth", 0, 3)
+            if n >= 1:
+                weigh(n - 1)
+            if q < len(jobs):
+                copy_job(q, 0, "S")
+                copy_job(q, 1, "S")
+            for key in step_outputs(n)[:1]:
+                emit(key, "S")
+            if n >= 2:
+                quantise(("vt", n - 2, 0), stage[("v", n - 2)][:], 256)
+            if n >= 2 and n % 2 == 0:
+                share = SHARE_EARLY if n <= 8 else SHARE_LATE
+                interleave((n - 2) // 2, "S", 0, share)
+                interleave((n - 2) // 2, "V", share, KP)
+
+        turn_v(14)
+        weigh(15)
+        copy_v(14, "S")
+        emit(("time", 2, 1), "S")
+        for a in (2, 3):
+            time_passes(2, a, 0, 2)
+        turn_v(15)
+        for j in (2, 3):
+            unit_passes(1, j, synth_ps, "synth", 0, 3)
+        quantise(("vt", 14, 0), stage[("v", 14)][:], 256)
+        interleave(7, "S", 0, SHARE_LAST)
+        interleave(7, "V", SHARE_LAST, KP)
+        copy_v(15, "S")
+        for j in range(2):
+            unit_passes(1, j, synth_ps, "synth", 3, 4)
+        emit(("time", 2, 2), "V")
+        quantise(("v", 7, 0), astage[7][:], KP)
+        emit(("time", 2, 3), "S")
+        quantise(("vt", 15, 0), stage[("v", 15)][:], 256)
+        for a in range(2):
+            time_passes(3, a, 0, 2)
+        emit(("unit", 1, 0), "S")
+        emit(("unit", 1, 1), "V")
+        for a in (2, 3):
+            time_passes(3, a, 0, 2)
+        for j in (2, 3):
+            unit_passes(1, j, synth_ps, "synth", 3, 4)
+        emit(("time", 3, 0), "S")
+        emit(("time", 3, 1), "V")
+        emit(("time", 3, 2), "S")
+        emit(("time", 3, 3), "V")
+        emit(("unit", 1, 2), "S")
+        emit(("unit", 1, 3), "V")

@@ -19,10 +19,10 @@ ACT = mybir.ActivationFunctionType
 P = 128
 KP = 512
 UNITS = 16
-AHEAD = 5
-SHARE_EARLY = 320
-SHARE_LATE = 192
-SHARE_LAST = 160
+HALF = 256
+CATCH_UP = 8
+LEAD = 3
+SHARES = ((128, 256), (128, 256))
 
 
 def tile_synthetic_control_placebos_s8_kernel(tc, y, w, z, prec, c_words, c_scales, win, out_0, out_1):
@@ -32,7 +32,7 @@ def tile_synthetic_control_placebos_s8_kernel(tc, y, w, z, prec, c_words, c_scal
         flow = ctx.enter_context(tc.tile_pool(name="flow", bufs=2))
         synth_ps = ctx.enter_context(tc.psum_pool(name="synth_ps", bufs=4))
         aux_ps = ctx.enter_context(tc.psum_pool(name="aux_ps", bufs=4))
-        ctx.enter_context(tc.manual_schedule())
+        ctx.enter_context(tc.manual_schedule(engines={mybir.EngineType.SP, mybir.EngineType.PE}))
 
         ident = keep.tile([P, P], F32, name="ident")
         make_identity(nc, ident[:])
@@ -45,22 +45,35 @@ def tile_synthetic_control_placebos_s8_kernel(tc, y, w, z, prec, c_words, c_scal
         rows, zt, pt, acc, dt, st, xt, astage = {}, {}, {}, {}, {}, {}, {}, {}
         banks, stage, quant, outs = {}, {}, {}, {}
 
-        def row_source(key):
-            kind, grp, i = key
-            if kind == "w":
-                return w[KP * grp + P * i : KP * grp + P * (i + 1), :]
-            src = y if kind == "y" else win
-            return src[KP * grp : KP * (grp + 1), :].rearrange("(m j) k -> m j k", j=4)[:, i, :]
+        def copy(eng, out, src):
+            if eng == "S":
+                nc.scalar.copy(out=out, in_=src)
+            elif eng == "G":
+                nc.gpsimd.tensor_scalar(out=out, in0=src, scalar1=1.0, scalar2=0.0, op0=ALU.mult, op1=ALU.add)
+            else:
+                nc.vector.tensor_copy(out=out, in_=src)
 
         def load_rows(key):
-            rows[key] = flow.tile([P, D], BF16, name="rows", bufs=14)
-            nc.sync.dma_start(out=rows[key][:], in_=row_source(key))
+            kind, i = key
+            if kind == "w":
+                src = w[P * i : P * (i + 1), :]
+            else:
+                full = y if kind == "y" else win
+                src = full[KP * (i // 4) : KP * (i // 4 + 1), :].rearrange("(m j) k -> m j k", j=4)[:, i % 4, :]
+            rows[key] = flow.tile([P, D], BF16, name="rows", bufs=10)
+            nc.sync.dma_start(out=rows[key][:], in_=src)
 
-        def load_cells(src, store, name, n):
-            gt, pb, h = n // 8, (n // 2) % 4, n % 2
-            store[n] = flow.tile([P, 2 * KP], BF16, name=name, bufs=7)
-            view = src[KP * gt : KP * (gt + 1), KP * pb : KP * (pb + 1)].rearrange("(m j) c -> m j c", j=4)
-            nc.sync.dma_start(out=store[n][:].rearrange("p (j c) -> p j c", j=2), in_=view[:, 2 * h : 2 * h + 2, :])
+        def cells(src, b):
+            gt, pb = b // 4, b % 4
+            return src[KP * gt : KP * (gt + 1), KP * pb : KP * (pb + 1)].rearrange("(m j) c -> m j c", j=4)
+
+        def load_z(b, jp):
+            zt[(b, jp)] = flow.tile([P, 2 * KP], BF16, name="zc", bufs=6)
+            nc.sync.dma_start(out=zt[(b, jp)][:].rearrange("p (j c) -> p j c", j=2), in_=cells(z, b)[:, 2 * jp : 2 * jp + 2, :])
+
+        def load_prec(b):
+            pt[b] = flow.tile([P, 4 * KP], BF16, name="pc", bufs=3)
+            nc.sync.dma_start(out=pt[b][:].rearrange("p (j c) -> p j c", j=4), in_=cells(prec, b))
 
         def load_c():
             nc.sync.dma_start(
@@ -73,258 +86,317 @@ def tile_synthetic_control_placebos_s8_kernel(tc, y, w, z, prec, c_words, c_scal
                     in_=c_scales.bitcast(I32)[:, 4 * q : 4 * q + 4, :].rearrange("g r n -> r g n"),
                 )
 
-        jobs = [("y", 0, 0), ("w", 0, 0), ("w", 0, 1), ("y", 0, 1)]
-        jobs = jobs + [("w", pb, g) for pb in range(1, 4) for g in range(2)]
-        jobs = jobs + [("y", 1, 0), ("y", 1, 1), ("win", 0, 0), ("win", 0, 1)]
-
         def slots(job):
-            kind, grp, i = job
-            if kind == "y":
-                return [((kind, grp, 2 * i + j), g) for j in range(2) for g in range(2)]
-            return [((kind, grp, a), i) for a in range(4)]
+            kind, i = job
+            if kind == "w":
+                return [((kind, 2 * i + a), g) for g in range(2) for a in range(2)]
+            return [((kind, 2 * i + a), g) for a in range(2) for g in range(2)]
 
-        def load_job(q):
-            for key, g in slots(jobs[q]):
-                if key not in rows:
-                    load_rows(key)
+        def load_job(job):
+            for a in range(2):
+                load_rows((job[0], 2 * job[1] + a))
 
-        def turn_job(q, half):
+        def turn_job(job, half):
             bank = aux_ps.tile([P, KP], F32, name="aux")
-            for s, (key, g) in enumerate(slots(jobs[q])[2 * half : 2 * half + 2]):
+            for s, (key, g) in enumerate(slots(job)[2 * half : 2 * half + 2]):
                 words = rows[key][:].bitcast(F32)
                 for u in range(2):
                     col = P * (2 * s + u)
                     nc.tensor.transpose(bank[:, col : col + P], words[:, 256 * g + u : 256 * (g + 1) : 2], ident[:])
-            banks[("job", q, half)] = bank
+            banks[(job, half)] = bank
 
-        def pair_copy(eng, dst, bank, order):
+        def pair_copy(eng, dst, bank):
             out = dst.bitcast(F32).rearrange("p (s m u) -> p s m u", s=2, u=2)
-            src = bank[:].rearrange(order, s=2, u=2)
-            if eng == "S":
-                nc.scalar.copy(out=out, in_=src)
-            else:
-                nc.vector.tensor_copy(out=out, in_=src)
+            copy(eng, out, bank[:].rearrange("p (s u m) -> p s m u", s=2, u=2))
 
-        def copy_job(q, half, eng):
+        def copy_job(job, half, eng):
             if half == 0:
-                stage[q] = flow.tile([P, 4 * KP], BF16, name="stage", bufs=3, align_bytes=64)
-            pair_copy(eng, stage[q][:, 1024 * half : 1024 * (half + 1)], banks[("job", q, half)], "p (s u m) -> p s m u")
+                stage[job] = flow.tile([P, 4 * KP], BF16, name="stage", bufs=3, align_bytes=64)
+            pair_copy(eng, stage[job][:, 1024 * half : 1024 * (half + 1)], banks[(job, half)])
 
         def quantise(key, src, width):
-            codes = keep.tile([P, width], U32, name="codes_%s_%d_%d" % key, align_bytes=64)
-            plane = keep.tile([P, width], U8, name="plane_%s_%d_%d" % key, align_bytes=64)
+            codes = keep.tile([P, width], U32, name="codes_%s_%d" % key, align_bytes=64)
+            plane = keep.tile([P, width], U8, name="plane_%s_%d" % key, align_bytes=64)
             nc.vector.quantize_mx(out=codes[:].bitcast(FP8X4), scales=plane[:], in_=src)
             quant[key] = (codes, plane)
 
-        def mx(out, left, lcol, right, start, stop):
+        def operand(key, lo, width):
+            codes, plane = quant[key]
+            return codes[:, lo : lo + width].bitcast(FP8X4), plane[:, lo : lo + width]
+
+        def mx(out, left, right, start, stop):
             nc.tensor.matmul_mx(
-                out=out,
-                lhsT=left[0][:, lcol : lcol + P].bitcast(FP8X4),
-                lhsT_scale=left[1][:, lcol : lcol + P],
-                rhs=right[0],
-                rhs_scale=right[1],
-                start=start,
-                stop=stop,
+                out=out, lhsT=left[0], lhsT_scale=left[1], rhs=right[0], rhs_scale=right[1], start=start, stop=stop
             )
 
-        def moving(key):
-            return (quant[key][0][:].bitcast(FP8X4), quant[key][1][:])
-
-        def synth(n):
-            gt, pb, h = n // 8, (n // 2) % 4, n % 2
+        def synth(n, jp):
+            bank = synth_ps.tile([P, KP], F32, name="synth")
             for j in range(2):
-                bank = synth_ps.tile([P, KP], F32, name="synth")
                 for g in range(2):
-                    mx(bank[:], quant[("y", gt, h)], P * (2 * j + g), moving(("w", pb, g)), g == 0, g == 1)
-                acc[(n, j)] = bank
+                    left = operand(("y", 2 * (n // 8) + jp), P * (2 * j + g), P)
+                    mx(bank[:, HALF * j : HALF * (j + 1)], left, operand(("w", n % 8), HALF * g, HALF), g == 0, g == 1)
+            acc[(n, jp)] = bank
 
-        def subtract(n):
-            dt[n] = flow.tile([P, 2 * KP], F32, name="gap", bufs=3)
-            for j in range(2):
-                cols = slice(KP * j, KP * (j + 1))
-                nc.vector.tensor_tensor(out=dt[n][:, cols], in0=acc[(n, j)][:], in1=zt[n][:, cols], op=ALU.subtract)
+        def subtract(n, jp):
+            if jp == 0:
+                dt[n] = flow.tile([P, 2 * KP], F32, name="gap", bufs=3)
+            zv = zt[(n // 2, jp)][:].rearrange("p (j c) -> p j c", j=2)
+            nc.vector.tensor_tensor(
+                out=dt[n][:, KP * jp : KP * (jp + 1)].rearrange("p (j c) -> p j c", j=2),
+                in0=acc[(n, jp)][:].rearrange("p (j c) -> p j c", j=2),
+                in1=zv[:, :, HALF * (n % 2) : HALF * (n % 2 + 1)],
+                op=ALU.subtract,
+            )
 
-        def square(n):
-            st[n] = flow.tile([P, 2 * KP], F32, name="sq", bufs=3)
+        def square(n, jp):
+            if jp == 0:
+                st[n] = flow.tile([P, 2 * KP], F32, name="sq", bufs=3)
+            cols = slice(KP * jp, KP * (jp + 1))
             nc.scalar.activation(
-                out=st[n][:].rearrange("p (u c e) -> p u c e", u=2, e=2),
-                in_=dt[n][:].rearrange("p (c u e) -> p u c e", u=2, e=2),
+                out=st[n][:, cols].rearrange("p (u c e) -> p u c e", u=2, e=2),
+                in_=dt[n][:, cols].rearrange("p (c u e) -> p u c e", u=2, e=2),
                 func=ACT.Square,
             )
 
-        def weigh(n):
-            b, h = n // 2, n % 2
-            if h == 0:
+        def weigh(n, lo, hi):
+            b, ph = n // 2, n % 2
+            if b not in xt:
                 xt[b] = flow.tile([P, 4 * KP], BF16, name="v", bufs=3)
-            nc.vector.tensor_tensor(
-                out=xt[b][:, 1024 * h : 1024 * (h + 1)].rearrange("p (u c e) -> p u c e", u=2, e=2),
-                in0=st[n][:].rearrange("p (u c e) -> p u c e", u=2, e=2),
-                in1=pt[n][:].rearrange("p (c u e) -> p u c e", u=2, e=2),
-                op=ALU.mult,
-            )
+            cols = slice(64 * ph, 64 * (ph + 1))
+            for u in range(2):
+                nc.vector.tensor_tensor(
+                    out=xt[b][:].rearrange("p (u q j m e) -> p u q j m e", u=2, q=2, j=2, e=2)[:, u, lo:hi, :, cols],
+                    in0=st[n][:].rearrange("p (q u j m e) -> p u q j m e", u=2, q=2, j=2, e=2)[:, u, lo:hi],
+                    in1=pt[b][:].rearrange("p (q j m u e) -> p u q j m e", u=2, q=2, j=2, e=2)[:, u, lo:hi, :, cols],
+                    op=ALU.mult,
+                )
 
-        def turn_v(n):
-            b, h = n // 2, n % 2
+        def turn_v(b, jp):
             bank = aux_ps.tile([P, KP], F32, name="aux")
             words = xt[b][:].bitcast(F32)
-            for i in range(4):
-                nc.tensor.transpose(bank[:, P * i : P * (i + 1)], words[:, KP * h + P * i : KP * h + P * (i + 1)], ident[:])
-            banks[("v", n)] = bank
+            for s in range(2):
+                for u in range(2):
+                    src = P * (4 * u + 2 * jp + s)
+                    nc.tensor.transpose(bank[:, P * (2 * s + u) : P * (2 * s + u + 1)], words[:, src : src + P], ident[:])
+            banks[("v", b, jp)] = bank
 
-        def copy_v(n, eng):
-            stage[("v", n)] = flow.tile([P, 2 * KP], BF16, name="vstage", bufs=3, align_bytes=64)
-            pair_copy(eng, stage[("v", n)][:], banks[("v", n)], "p (u s m) -> p s m u")
+        def copy_v(b, jp, eng):
+            stage[("v", b, jp)] = flow.tile([P, 2 * KP], BF16, name="vstage", bufs=3, align_bytes=64)
+            pair_copy(eng, stage[("v", b, jp)][:], banks[("v", b, jp)])
 
-        def interleave(b, eng, lo, hi):
-            if b not in astage:
-                astage[b] = flow.tile([P, 4 * KP], BF16, name="astage", bufs=2, align_bytes=64)
-            src = xt[b][:].rearrange("p (h u j c i) -> p u c h j i", h=2, u=2, j=2, i=4)
-            dst = astage[b][:].rearrange("p (u c i h j) -> p u c h j i", u=2, i=4, h=2, j=2)
-            for u in range(2):
-                c0, c1 = max(lo - 256 * u, 0) // 4, min(hi - 256 * u, 256) // 4
+        def quantise_v(b, jp):
+            quantise(("vt", 2 * b + jp), stage[("v", b, jp)][:], HALF)
+
+        def interleave(n, eng, lo, hi):
+            k, gt = n % 8, n // 8
+            if k not in astage:
+                astage[k] = flow.tile([P, 4 * KP], BF16, name="astage", bufs=8, align_bytes=64)
+            src = xt[n // 2][:].rearrange("p (u j h c i) -> p h u c j i", u=2, j=4, h=2, i=4)[:, n % 2]
+            dst = astage[k][:].rearrange("p (g u c i j) -> p g u c j i", g=2, u=2, i=4, j=4)[:, gt]
+            if (lo, hi) == (0, HALF) and eng != "G":
+                copy(eng, dst, src)
+                return
+            for u in (1, 0):
+                c0, c1 = max(lo - P * u, 0) // 4, min(hi - P * u, P) // 4
                 if c1 > c0:
-                    if eng == "S":
-                        nc.scalar.copy(out=dst[:, u, c0:c1], in_=src[:, u, c0:c1])
-                    else:
-                        nc.vector.tensor_copy(out=dst[:, u, c0:c1], in_=src[:, u, c0:c1])
+                    copy(eng, dst[:, u, c0:c1], src[:, u, c0:c1])
 
         def unit_passes(gt, j, pool, name, first, last):
             if first == 0:
                 outs[("unit", gt, j)] = pool.tile([P, KP], F32, name=name)
             for pb in range(first, last):
                 rhs = (c_codes[:, 2 * G * pb : 2 * G * (pb + 1)].bitcast(FP4X4), c_plane[:, G * pb : G * (pb + 1)])
-                mx(outs[("unit", gt, j)][:], quant[("vt", 8 * gt + 2 * pb + j // 2, 0)], P * (j % 2), rhs, pb == 0, pb == 3)
+                left = operand(("vt", 8 * gt + 2 * pb + j // 2), P * (j % 2), P)
+                mx(outs[("unit", gt, j)][:], left, rhs, pb == 0, pb == 3)
 
-        def time_passes(pb, a, first, last):
-            if first == 0:
-                outs[("time", pb, a)] = aux_ps.tile([P, KP], F32, name="aux")
-            for gt in range(first, last):
-                mx(outs[("time", pb, a)][:], quant[("win", 0, gt)], P * a, moving(("v", 4 * gt + pb, 0)), gt == 0, gt == 1)
+        def time_passes(k, ap):
+            bank = aux_ps.tile([P, KP], F32, name="aux")
+            for a in range(2):
+                for gt in range(2):
+                    left = operand(("win", ap), P * (2 * a + gt), P)
+                    mx(bank[:, HALF * a : HALF * (a + 1)], left, operand(("v", k), HALF * gt, HALF), gt == 0, gt == 1)
+            outs[("time", k, ap)] = bank
 
         def emit(key, eng):
             kind, grp, i = key
             res = flow.tile([P, KP], F32, name="res", bufs=8)
             if kind == "unit":
-                out, src = res[:], outs[key][:]
+                copy(eng, res[:], outs[key][:])
                 dest = out_0[KP * grp : KP * (grp + 1), :].rearrange("(m j) n -> m j n", j=4)[:, i, :]
+                nc.sync.dma_start(out=dest, in_=res[:])
             else:
-                out = res[:].rearrange("p (c u e) -> p c u e", u=2, e=2)
-                src = outs[key][:].rearrange("p (u c e) -> p c u e", u=2, e=2)
-                dest = out_1.rearrange("(m a) n -> m a n", a=4)[:, i, KP * grp : KP * (grp + 1)]
-            if eng == "S":
-                nc.scalar.copy(out=out, in_=src)
-            else:
-                nc.vector.tensor_copy(out=out, in_=src)
-            nc.sync.dma_start(out=dest, in_=res[:])
+                copy(
+                    eng,
+                    res[:].rearrange("p (a c u e) -> p a c u e", a=2, u=2, e=2),
+                    outs[key][:].rearrange("p (a u c e) -> p a c u e", a=2, u=2, e=2),
+                )
+                dest = out_1.rearrange("(m a) n -> m a n", a=4)[:, 2 * i : 2 * i + 2, HALF * grp : HALF * (grp + 1)]
+                nc.sync.dma_start(out=dest, in_=res[:].rearrange("p (a c) -> p a c", a=2))
 
-        def step_outputs(n):
-            if n in (9, 10):
-                return [("unit", 0, 2 * (n - 9) + i) for i in range(2)]
-            if 11 <= n <= 16:
-                return [("time", (n - 11) // 2, 2 * ((n - 11) % 2) + i) for i in range(2)]
-            return []
+        later_jobs = [("w", i) for i in range(3, 8)] + [("y", 2), ("y", 3), ("win", 0), ("win", 1)]
 
-        for q in range(4):
-            load_job(q)
-        load_cells(z, zt, "zc", 0)
-        load_cells(prec, pt, "pc", 0)
-        load_job(4)
-        load_cells(z, zt, "zc", 1)
-        for q in range(4):
-            for half in range(2):
-                turn_job(q, half)
-                copy_job(q, half, "SV"[half])
-            if q > 0:
-                quantise(jobs[q - 1], stage[q - 1][:], KP)
-        load_cells(prec, pt, "pc", 1)
-        load_job(6)
-        for n in range(2, AHEAD):
-            load_cells(z, zt, "zc", n)
-            load_cells(prec, pt, "pc", n)
-        synth(0)
-        for half in range(2):
-            turn_job(4, half)
-            copy_job(4, half, "S")
-        quantise(jobs[3], stage[3][:], KP)
-
-        for n in range(UNITS):
-            q = n + 5
-            if n + AHEAD < UNITS:
-                load_cells(z, zt, "zc", n + AHEAD)
-                load_cells(prec, pt, "pc", n + AHEAD)
-            if q + 3 < len(jobs):
-                load_job(q + 3)
-            if n == 4:
+        def loads(need):
+            if need % 2 == 0 and 0 < need < UNITS:
+                load_z(need // 2, 0)
+                load_z(need // 2, 1)
+            if need % 2 == 1 and need < UNITS:
+                load_prec(need // 2)
+            if need < len(later_jobs):
+                load_job(later_jobs[need])
+            if need == 9:
                 load_c()
-            if n >= 2:
-                turn_v(n - 2)
-            if q < len(jobs):
-                turn_job(q, 0)
-                turn_job(q, 1)
-            subtract(n)
-            if n >= 2:
-                copy_v(n - 2, "S")
-            for key in step_outputs(n - 1)[1:]:
-                emit(key, "S")
-            if q - 1 < len(jobs):
-                quantise(jobs[q - 1], stage[q - 1][:], KP)
-            if n >= 3 and n % 2 == 1:
-                quantise(("v", (n - 3) // 2, 0), astage[(n - 3) // 2][:], KP)
-            square(n)
-            if n + 1 < UNITS:
-                synth(n + 1)
-            for kind, grp, i in step_outputs(n):
-                if kind == "unit":
-                    unit_passes(grp, i, aux_ps, "aux", 0, 4)
-                else:
-                    time_passes(grp, i, 0, 2)
-            if n + 1 == UNITS:
-                for j in range(2):
-                    unit_passes(1, j, synth_ps, "synth", 0, 3)
-            if n >= 1:
-                weigh(n - 1)
-            if q < len(jobs):
-                copy_job(q, 0, "S")
-                copy_job(q, 1, "S")
-            for key in step_outputs(n)[:1]:
-                emit(key, "S")
-            if n >= 2:
-                quantise(("vt", n - 2, 0), stage[("v", n - 2)][:], 256)
-            if n >= 2 and n % 2 == 0:
-                share = SHARE_EARLY if n <= 8 else SHARE_LATE
-                interleave((n - 2) // 2, "S", 0, share)
-                interleave((n - 2) // 2, "V", share, KP)
 
-        turn_v(14)
-        weigh(15)
-        copy_v(14, "S")
-        emit(("time", 2, 1), "S")
-        for a in (2, 3):
-            time_passes(2, a, 0, 2)
-        turn_v(15)
+        def spread(n, eng):
+            act_end, dve_end = SHARES[n // 8]
+            lo, hi = {"S": (0, act_end), "V": (act_end, dve_end), "G": (dve_end, HALF)}[eng]
+            if hi > lo:
+                interleave(n, eng, lo, hi)
+
+        load_job(("y", 0))
+        load_job(("w", 0))
+        load_job(("y", 1))
+        load_z(0, 0)
+        load_job(("w", 1))
+        load_z(0, 1)
+        load_job(("w", 2))
+        for job in (("y", 0), ("w", 0)):
+            for half in range(2):
+                turn_job(job, half)
+                copy_job(job, half, "SV"[half])
+            quantise(job, stage[job][:], KP)
+        for half in range(2):
+            turn_job(("y", 1), half)
+            copy_job(("y", 1), half, "S")
+        for need in range(LEAD):
+            loads(need)
+        synth(0, 0)
+        quantise(("y", 1), stage[("y", 1)][:], KP)
+        for half in range(2):
+            turn_job(("w", 1), half)
+        copy_job(("w", 1), 0, "S")
+        synth(0, 1)
+        subtract(0, 0)
+        copy_job(("w", 1), 1, "V")
+        square(0, 0)
+        for half in range(2):
+            turn_job(("w", 2), half)
+        subtract(0, 1)
+        quantise(("w", 1), stage[("w", 1)][:], KP)
+        copy_job(("w", 2), 0, "S")
+        copy_job(("w", 2), 1, "V")
+        pending = [("w", 2)]
+        turned = []
+
+        for n in range(9):
+            loads(n + LEAD)
+            job = later_jobs[n]
+            synth(n + 1, 0)
+            turn_job(job, 0)
+            if n >= 2:
+                spread(n - 2, "S")
+            if n > 0:
+                subtract(n, 0)
+                square(n, 0)
+                subtract(n, 1)
+            quantise(pending[0], stage[pending[0]][:], KP)
+            pending = [job]
+            synth(n + 1, 1)
+            copy_job(job, 0, "S")
+            square(n, 1)
+            done = turned
+            turned = [divmod(n - 3, 2)] if n >= 3 else []
+            for b, jp in turned:
+                turn_v(b, jp)
+                copy_v(b, jp, "S")
+            turn_job(job, 1)
+            copy_job(job, 1, "S")
+            for b, jp in done:
+                quantise_v(b, jp)
+            if n >= 2:
+                spread(n - 2, "V")
+            if n >= 1:
+                weigh(n - 1, 0, 2)
+                spread(n - 1, "G")
+        quantise_v(2, 1)
+        spread(7, "S")
+        spread(7, "V")
+        weigh(8, 0, 2)
+        spread(8, "G")
+        turn_v(3, 0)
+        turned = [(3, 0)]
+
+        for n in range(9, UNITS):
+            loads(n + LEAD)
+            if n + 1 < UNITS:
+                synth(n + 1, 0)
+                synth(n + 1, 1)
+            else:
+                for j in range(2):
+                    unit_passes(1, j, synth_ps, "synth", 0, 2)
+            if n > 9:
+                time_passes(n - 10, 0)
+                time_passes(n - 10, 1)
+            for b, jp in turned:
+                copy_v(b, jp, "S")
+            spread(n - 1, "S")
+            subtract(n, 0)
+            square(n, 0)
+            subtract(n, 1)
+            square(n, 1)
+            if 10 <= n < 14:
+                unit_passes(0, n - 10, aux_ps, "aux", 0, 4)
+            if n == 15:
+                for j in (2, 3):
+                    unit_passes(1, j, synth_ps, "synth", 0, 2)
+            for job in pending:
+                quantise(job, stage[job][:], KP)
+            pending = []
+            spread(n - 1, "V")
+            for b, jp in turned:
+                quantise_v(b, jp)
+            if n > 9:
+                emit(("time", n - 10, 0), "S")
+            turned = [divmod(n - 2, 2)]
+            for b, jp in turned:
+                turn_v(b, jp)
+            quantise(("v", n - 9), astage[n - 9][:], KP)
+            if n > 9:
+                emit(("time", n - 10, 1), "S")
+            if 10 <= n < 14:
+                emit(("unit", 0, n - 10), "S")
+            if n + 1 < UNITS:
+                weigh(n, 0, 2)
+                spread(n, "G")
+
+        for j in range(2):
+            unit_passes(1, j, synth_ps, "synth", 2, 3)
+        time_passes(6, 0)
+        copy_v(6, 1, "S")
+        weigh(15, 0, 1)
+        turn_v(7, 0)
+        weigh(15, 1, 2)
+        emit(("time", 6, 0), "S")
+        turn_v(7, 1)
+        time_passes(6, 1)
+        quantise_v(6, 1)
+        copy_v(7, 0, "S")
+        interleave(15, "V", 0, HALF)
+        copy_v(7, 1, "S")
+        quantise_v(7, 0)
         for j in (2, 3):
-            unit_passes(1, j, synth_ps, "synth", 0, 3)
-        quantise(("vt", 14, 0), stage[("v", 14)][:], 256)
-        interleave(7, "S", 0, SHARE_LAST)
-        interleave(7, "V", SHARE_LAST, KP)
-        copy_v(15, "S")
+            unit_passes(1, j, synth_ps, "synth", 2, 3)
+        quantise(("v", 7), astage[7][:], KP)
+        emit(("time", 6, 1), "S")
         for j in range(2):
             unit_passes(1, j, synth_ps, "synth", 3, 4)
-        emit(("time", 2, 2), "V")
-        quantise(("v", 7, 0), astage[7][:], KP)
-        emit(("time", 2, 3), "S")
-        quantise(("vt", 15, 0), stage[("v", 15)][:], 256)
-        for a in range(2):
-            time_passes(3, a, 0, 2)
-        emit(("unit", 1, 0), "S")
-        emit(("unit", 1, 1), "V")
-        for a in (2, 3):
-            time_passes(3, a, 0, 2)
+        quantise_v(7, 1)
+        time_passes(7, 0)
+        time_passes(7, 1)
         for j in (2, 3):
             unit_passes(1, j, synth_ps, "synth", 3, 4)
-        emit(("time", 3, 0), "S")
-        emit(("time", 3, 1), "V")
-        emit(("time", 3, 2), "S")
-        emit(("time", 3, 3), "V")
-        emit(("unit", 1, 2), "S")
-        emit(("unit", 1, 3), "V")
+        emit(("unit", 1, 0), "V")
+        emit(("unit", 1, 1), "S")
+        emit(("time", 7, 0), "V")
+        emit(("time", 7, 1), "S")
+        emit(("unit", 1, 2), "V")
+        emit(("unit", 1, 3), "S")

@@ -22,7 +22,6 @@ UNITS = 16
 HALF = 256
 CATCH_UP = 8
 LEAD = 3
-SHARES = ((128, 256), (128, 256))
 
 
 def tile_synthetic_control_placebos_s8_kernel(tc, y, w, z, prec, c_words, c_scales, win, out_0, out_1):
@@ -32,7 +31,7 @@ def tile_synthetic_control_placebos_s8_kernel(tc, y, w, z, prec, c_words, c_scal
         flow = ctx.enter_context(tc.tile_pool(name="flow", bufs=2))
         synth_ps = ctx.enter_context(tc.psum_pool(name="synth_ps", bufs=4))
         aux_ps = ctx.enter_context(tc.psum_pool(name="aux_ps", bufs=4))
-        ctx.enter_context(tc.manual_schedule(engines={mybir.EngineType.SP, mybir.EngineType.PE}))
+        ctx.enter_context(tc.manual_schedule(engines={mybir.EngineType.SP, mybir.EngineType.PE, mybir.EngineType.DVE, mybir.EngineType.Pool}))
 
         ident = keep.tile([P, P], F32, name="ident")
         make_identity(nc, ident[:])
@@ -48,8 +47,6 @@ def tile_synthetic_control_placebos_s8_kernel(tc, y, w, z, prec, c_words, c_scal
         def copy(eng, out, src):
             if eng == "S":
                 nc.scalar.copy(out=out, in_=src)
-            elif eng == "G":
-                nc.gpsimd.tensor_scalar(out=out, in0=src, scalar1=1.0, scalar2=0.0, op0=ALU.mult, op1=ALU.add)
             else:
                 nc.vector.tensor_copy(out=out, in_=src)
 
@@ -71,9 +68,10 @@ def tile_synthetic_control_placebos_s8_kernel(tc, y, w, z, prec, c_words, c_scal
             zt[(b, jp)] = flow.tile([P, 2 * KP], BF16, name="zc", bufs=6)
             nc.sync.dma_start(out=zt[(b, jp)][:].rearrange("p (j c) -> p j c", j=2), in_=cells(z, b)[:, 2 * jp : 2 * jp + 2, :])
 
-        def load_prec(b):
-            pt[b] = flow.tile([P, 4 * KP], BF16, name="pc", bufs=3)
-            nc.sync.dma_start(out=pt[b][:].rearrange("p (j c) -> p j c", j=4), in_=cells(prec, b))
+        def load_prec(n):
+            pt[n] = flow.tile([P, 4 * HALF], BF16, name="pc", bufs=6)
+            view = cells(prec, n // 2)[:, :, HALF * (n % 2) : HALF * (n % 2 + 1)]
+            nc.sync.dma_start(out=pt[n][:].rearrange("p (j c) -> p j c", j=4), in_=view)
 
         def load_c():
             nc.sync.dma_start(
@@ -163,13 +161,12 @@ def tile_synthetic_control_placebos_s8_kernel(tc, y, w, z, prec, c_words, c_scal
             if b not in xt:
                 xt[b] = flow.tile([P, 4 * KP], BF16, name="v", bufs=3)
             cols = slice(64 * ph, 64 * (ph + 1))
-            for u in range(2):
-                nc.vector.tensor_tensor(
-                    out=xt[b][:].rearrange("p (u q j m e) -> p u q j m e", u=2, q=2, j=2, e=2)[:, u, lo:hi, :, cols],
-                    in0=st[n][:].rearrange("p (q u j m e) -> p u q j m e", u=2, q=2, j=2, e=2)[:, u, lo:hi],
-                    in1=pt[b][:].rearrange("p (q j m u e) -> p u q j m e", u=2, q=2, j=2, e=2)[:, u, lo:hi, :, cols],
-                    op=ALU.mult,
-                )
+            nc.vector.tensor_tensor(
+                out=xt[b][:].rearrange("p (u q j m e) -> p u q j m e", u=2, q=2, j=2, e=2)[:, :, lo:hi, :, cols],
+                in0=st[n][:].rearrange("p (q u j m e) -> p u q j m e", u=2, q=2, j=2, e=2)[:, :, lo:hi],
+                in1=pt[n][:].rearrange("p (q j m u e) -> p u q j m e", u=2, q=2, j=2, e=2)[:, :, lo:hi],
+                op=ALU.mult,
+            )
 
         def turn_v(b, jp):
             bank = aux_ps.tile([P, KP], F32, name="aux")
@@ -187,19 +184,18 @@ def tile_synthetic_control_placebos_s8_kernel(tc, y, w, z, prec, c_words, c_scal
         def quantise_v(b, jp):
             quantise(("vt", 2 * b + jp), stage[("v", b, jp)][:], HALF)
 
-        def interleave(n, eng, lo, hi):
+        def interleave(n, eng, u):
             k, gt = n % 8, n // 8
             if k not in astage:
                 astage[k] = flow.tile([P, 4 * KP], BF16, name="astage", bufs=8, align_bytes=64)
-            src = xt[n // 2][:].rearrange("p (u j h c i) -> p h u c j i", u=2, j=4, h=2, i=4)[:, n % 2]
-            dst = astage[k][:].rearrange("p (g u c i j) -> p g u c j i", g=2, u=2, i=4, j=4)[:, gt]
-            if (lo, hi) == (0, HALF) and eng != "G":
+            if eng == "G":
+                src = xt[n // 2][:].rearrange("p (u j h c) -> p h u c j", u=2, j=4, h=2)[:, n % 2, u]
+                dst = astage[k][:].rearrange("p (g u c j) -> p g u c j", g=2, u=2, j=4)[:, gt, u]
+                nc.gpsimd.tensor_scalar(out=dst, in0=src, scalar1=1.0, scalar2=0.0, op0=ALU.mult, op1=ALU.add)
+            else:
+                src = xt[n // 2][:].rearrange("p (u j h c i) -> p h u c j i", u=2, j=4, h=2, i=4)[:, n % 2, u]
+                dst = astage[k][:].rearrange("p (g u c i j) -> p g u c j i", g=2, u=2, i=4, j=4)[:, gt, u]
                 copy(eng, dst, src)
-                return
-            for u in (1, 0):
-                c0, c1 = max(lo - P * u, 0) // 4, min(hi - P * u, P) // 4
-                if c1 > c0:
-                    copy(eng, dst[:, u, c0:c1], src[:, u, c0:c1])
 
         def unit_passes(gt, j, pool, name, first, last):
             if first == 0:
@@ -239,18 +235,12 @@ def tile_synthetic_control_placebos_s8_kernel(tc, y, w, z, prec, c_words, c_scal
             if need % 2 == 0 and 0 < need < UNITS:
                 load_z(need // 2, 0)
                 load_z(need // 2, 1)
-            if need % 2 == 1 and need < UNITS:
-                load_prec(need // 2)
+            if 0 < need <= UNITS:
+                load_prec(need - 1)
             if need < len(later_jobs):
                 load_job(later_jobs[need])
             if need == 9:
                 load_c()
-
-        def spread(n, eng):
-            act_end, dve_end = SHARES[n // 8]
-            lo, hi = {"S": (0, act_end), "V": (act_end, dve_end), "G": (dve_end, HALF)}[eng]
-            if hi > lo:
-                interleave(n, eng, lo, hi)
 
         load_job(("y", 0))
         load_job(("w", 0))
@@ -284,46 +274,43 @@ def tile_synthetic_control_placebos_s8_kernel(tc, y, w, z, prec, c_words, c_scal
         quantise(("w", 1), stage[("w", 1)][:], KP)
         copy_job(("w", 2), 0, "S")
         copy_job(("w", 2), 1, "V")
-        pending = [("w", 2)]
-        turned = []
+        pending = ("w", 2)
 
         for n in range(9):
             loads(n + LEAD)
             job = later_jobs[n]
-            synth(n + 1, 0)
             turn_job(job, 0)
             if n >= 2:
-                spread(n - 2, "S")
+                interleave(n - 2, "S", 0)
             if n > 0:
                 subtract(n, 0)
                 square(n, 0)
                 subtract(n, 1)
-            quantise(pending[0], stage[pending[0]][:], KP)
-            pending = [job]
-            synth(n + 1, 1)
-            copy_job(job, 0, "S")
-            square(n, 1)
-            done = turned
-            turned = [divmod(n - 3, 2)] if n >= 3 else []
-            for b, jp in turned:
-                turn_v(b, jp)
-                copy_v(b, jp, "S")
+            if n >= 4 and n % 2 == 1:
+                copy_v(*divmod(n - 4, 2), "V")
+            quantise(pending, stage[pending][:], KP)
+            pending = job
             turn_job(job, 1)
+            if n >= 3:
+                turn_v(*divmod(n - 3, 2))
+            synth(n + 1, 0)
+            synth(n + 1, 1)
+            square(n, 1)
+            copy_job(job, 0, "S")
             copy_job(job, 1, "S")
-            for b, jp in done:
-                quantise_v(b, jp)
-            if n >= 2:
-                spread(n - 2, "V")
+            if n >= 4:
+                quantise_v(*divmod(n - 4, 2))
+            if n >= 3 and n % 2 == 1:
+                copy_v(*divmod(n - 3, 2), "S")
             if n >= 1:
                 weigh(n - 1, 0, 2)
-                spread(n - 1, "G")
-        quantise_v(2, 1)
-        spread(7, "S")
-        spread(7, "V")
-        weigh(8, 0, 2)
-        spread(8, "G")
+                interleave(n - 1, "G", 1)
         turn_v(3, 0)
-        turned = [(3, 0)]
+        interleave(7, "S", 0)
+        copy_v(2, 1, "S")
+        copy_v(3, 0, "S")
+        weigh(8, 0, 2)
+        interleave(8, "G", 1)
 
         for n in range(9, UNITS):
             loads(n + LEAD)
@@ -336,67 +323,64 @@ def tile_synthetic_control_placebos_s8_kernel(tc, y, w, z, prec, c_words, c_scal
             if n > 9:
                 time_passes(n - 10, 0)
                 time_passes(n - 10, 1)
-            for b, jp in turned:
-                copy_v(b, jp, "S")
-            spread(n - 1, "S")
+            interleave(n - 1, "S", 0)
             subtract(n, 0)
             square(n, 0)
             subtract(n, 1)
             square(n, 1)
+            if 11 <= n < 15:
+                emit(("unit", 0, n - 11), "V")
+            if n == 9:
+                quantise(pending, stage[pending][:], KP)
+                quantise_v(2, 1)
+                quantise_v(3, 0)
+            if n >= 10:
+                copy_v(*divmod(n - 3, 2), "S")
+            if n >= 11:
+                quantise_v(*divmod(n - 4, 2))
             if 10 <= n < 14:
                 unit_passes(0, n - 10, aux_ps, "aux", 0, 4)
             if n == 15:
                 for j in (2, 3):
                     unit_passes(1, j, synth_ps, "synth", 0, 2)
-            for job in pending:
-                quantise(job, stage[job][:], KP)
-            pending = []
-            spread(n - 1, "V")
-            for b, jp in turned:
-                quantise_v(b, jp)
             if n > 9:
                 emit(("time", n - 10, 0), "S")
-            turned = [divmod(n - 2, 2)]
-            for b, jp in turned:
-                turn_v(b, jp)
+            turn_v(*divmod(n - 2, 2))
             quantise(("v", n - 9), astage[n - 9][:], KP)
             if n > 9:
                 emit(("time", n - 10, 1), "S")
-            if 10 <= n < 14:
-                emit(("unit", 0, n - 10), "S")
             if n + 1 < UNITS:
                 weigh(n, 0, 2)
-                spread(n, "G")
+                interleave(n, "G", 1)
 
-        for j in range(2):
-            unit_passes(1, j, synth_ps, "synth", 2, 3)
         time_passes(6, 0)
         copy_v(6, 1, "S")
-        weigh(15, 0, 1)
+        weigh(15, 0, 2)
         turn_v(7, 0)
-        weigh(15, 1, 2)
-        emit(("time", 6, 0), "S")
         turn_v(7, 1)
-        time_passes(6, 1)
-        quantise_v(6, 1)
+        quantise_v(6, 0)
+        interleave(15, "V", 1)
         copy_v(7, 0, "S")
-        interleave(15, "V", 0, HALF)
-        copy_v(7, 1, "S")
-        quantise_v(7, 0)
-        for j in (2, 3):
+        interleave(15, "V", 0)
+        for j in range(2):
             unit_passes(1, j, synth_ps, "synth", 2, 3)
-        quantise(("v", 7), astage[7][:], KP)
-        emit(("time", 6, 1), "S")
+        time_passes(6, 1)
+        emit(("time", 6, 0), "S")
+        quantise_v(6, 1)
+        quantise_v(7, 0)
         for j in range(2):
             unit_passes(1, j, synth_ps, "synth", 3, 4)
-        quantise_v(7, 1)
+        quantise(("v", 7), astage[7][:], KP)
+        emit(("time", 6, 1), "S")
+        copy_v(7, 1, "V")
         time_passes(7, 0)
         time_passes(7, 1)
+        emit(("unit", 1, 0), "S")
+        emit(("unit", 1, 1), "V")
+        quantise_v(7, 1)
         for j in (2, 3):
-            unit_passes(1, j, synth_ps, "synth", 3, 4)
-        emit(("unit", 1, 0), "V")
-        emit(("unit", 1, 1), "S")
-        emit(("time", 7, 0), "V")
-        emit(("time", 7, 1), "S")
-        emit(("unit", 1, 2), "V")
-        emit(("unit", 1, 3), "S")
+            unit_passes(1, j, synth_ps, "synth", 2, 4)
+        emit(("time", 7, 0), "S")
+        emit(("time", 7, 1), "V")
+        emit(("unit", 1, 2), "S")
+        emit(("unit", 1, 3), "V")

@@ -3,8 +3,8 @@ from contextlib import ExitStack
 import concourse.mybir as mybir
 from concourse.masks import make_identity
 
-T, D, NP, G, R = 1024, 1024, 2048, 512, 512
-FLOPS = 2 * T * D * NP + 2 * T * NP * G + 2 * R * T * NP
+PERIODS, DONORS, PLACEBOS, UNIT_CONTRASTS, TIME_CONTRASTS = 1024, 1024, 2048, 512, 512
+FLOPS = 2 * PERIODS * PLACEBOS * (DONORS + UNIT_CONTRASTS + TIME_CONTRASTS)
 
 F32 = mybir.dt.float32
 BF16 = mybir.dt.bfloat16
@@ -15,13 +15,18 @@ FP8X4 = mybir.dt.float8_e4m3fn_x4
 FP4X4 = mybir.dt.float4_e2m1fn_x4
 ALU = mybir.AluOpType
 ACT = mybir.ActivationFunctionType
+ENGINE = mybir.EngineType
 
 P = 128
-KP = 512
+PASS = 512
+BANK = 512
+STRIP = 256
+PASS_WORDS = PASS // 2
 UNITS = 16
-HALF = 256
-CATCH_UP = 8
+STRIPS = 8
+C_PASSES = PLACEBOS // PASS
 LEAD = 3
+VECTOR, SCALAR, GPSIMD = "vector", "scalar", "gpsimd"
 
 
 def tile_synthetic_control_placebos_s8_kernel(tc, y, w, z, prec, c_words, c_scales, win, out_0, out_1):
@@ -31,215 +36,252 @@ def tile_synthetic_control_placebos_s8_kernel(tc, y, w, z, prec, c_words, c_scal
         flow = ctx.enter_context(tc.tile_pool(name="flow", bufs=2))
         synth_ps = ctx.enter_context(tc.psum_pool(name="synth_ps", bufs=4))
         aux_ps = ctx.enter_context(tc.psum_pool(name="aux_ps", bufs=4))
-        ctx.enter_context(tc.manual_schedule(engines={mybir.EngineType.SP, mybir.EngineType.PE, mybir.EngineType.DVE, mybir.EngineType.Pool}))
+        ctx.enter_context(tc.manual_schedule(engines={ENGINE.SP, ENGINE.PE, ENGINE.DVE, ENGINE.Pool}))
 
+        ident_root = keep.tile([P, P], F32, name="ident_root")
+        make_identity(nc, ident_root[:])
         ident = keep.tile([P, P], F32, name="ident")
-        make_identity(nc, ident[:])
-        warm = keep.tile([P, 8], F32, name="warm")
-        nc.scalar.activation(out=warm[:], in_=ident[:, 0:8], func=ACT.Square)
-        c_plane = keep.tile([P, 4 * G], U8, name="c_plane", align_bytes=64)
-        nc.gpsimd.memset(c_plane[:].bitcast(U32), 0)
-        c_codes = keep.tile([P, 4 * 2 * G], U8, name="c_codes", align_bytes=64)
+        nc.scalar.activation(out=ident[:], in_=ident_root[:], func=ACT.Square)
+        c_scale_tile = keep.tile([P, C_PASSES * UNIT_CONTRASTS], U8, name="c_scale_tile", align_bytes=64)
+        nc.gpsimd.memset(c_scale_tile[:].bitcast(U32), 0)
+        c_code_tile = keep.tile([P, C_PASSES * 2 * UNIT_CONTRASTS], U8, name="c_code_tile", align_bytes=64)
 
-        rows, zt, pt, acc, dt, st, xt, astage = {}, {}, {}, {}, {}, {}, {}, {}
-        banks, stage, quant, outs = {}, {}, {}, {}
+        rows, z_tiles, prec_tiles = {}, {}, {}
+        synth_banks, gaps, squares, v_tiles = {}, {}, {}, {}
+        turned, staged, quantised, results = {}, {}, {}, {}
 
-        def copy(eng, out, src):
-            if eng == "S":
+        def copy(engine, out, src):
+            if engine == SCALAR:
                 nc.scalar.copy(out=out, in_=src)
             else:
                 nc.vector.tensor_copy(out=out, in_=src)
 
-        def load_rows(key):
-            kind, i = key
-            if kind == "w":
-                src = w[P * i : P * (i + 1), :]
-            else:
-                full = y if kind == "y" else win
-                src = full[KP * (i // 4) : KP * (i // 4 + 1), :].rearrange("(m j) k -> m j k", j=4)[:, i % 4, :]
-            rows[key] = flow.tile([P, D], BF16, name="rows", bufs=10)
-            nc.sync.dma_start(out=rows[key][:], in_=src)
 
-        def cells(src, b):
-            gt, pb = b // 4, b % 4
-            return src[KP * gt : KP * (gt + 1), KP * pb : KP * (pb + 1)].rearrange("(m j) c -> m j c", j=4)
+        def load_job(job):
+            kind, index = job
+            for i in (2 * index, 2 * index + 1):
+                if kind == "w":
+                    src = w[P * i : P * (i + 1), :]
+                else:
+                    run = (y if kind == "y" else win)[PASS * (i // 4) : PASS * (i // 4 + 1), :]
+                    src = run.rearrange("(m j) k -> m j k", j=4)[:, i % 4, :]
+                rows[(kind, i)] = flow.tile([P, DONORS], BF16, name="rows", bufs=10)
+                nc.sync.dma_start(out=rows[(kind, i)][:], in_=src)
 
-        def load_z(b, jp):
-            zt[(b, jp)] = flow.tile([P, 2 * KP], BF16, name="zc", bufs=6)
-            nc.sync.dma_start(out=zt[(b, jp)][:].rearrange("p (j c) -> p j c", j=2), in_=cells(z, b)[:, 2 * jp : 2 * jp + 2, :])
+        def block_view(src, block):
+            group, c_pass = divmod(block, C_PASSES)
+            cells = src[PASS * group : PASS * (group + 1), PASS * c_pass : PASS * (c_pass + 1)]
+            return cells.rearrange("(m j) c -> m j c", j=4)
 
-        def load_prec(n):
-            pt[n] = flow.tile([P, 4 * HALF], BF16, name="pc", bufs=6)
-            view = cells(prec, n // 2)[:, :, HALF * (n % 2) : HALF * (n % 2 + 1)]
-            nc.sync.dma_start(out=pt[n][:].rearrange("p (j c) -> p j c", j=4), in_=view)
+        def load_z(block, pair):
+            z_tiles[(block, pair)] = flow.tile([P, 2 * PASS], BF16, name="z_tile", bufs=6)
+            nc.sync.dma_start(
+                out=z_tiles[(block, pair)][:].rearrange("p (j c) -> p j c", j=2),
+                in_=block_view(z, block)[:, 2 * pair : 2 * pair + 2, :],
+            )
+
+        def load_prec(unit):
+            prec_tiles[unit] = flow.tile([P, 4 * STRIP], BF16, name="prec_tile", bufs=6)
+            nc.sync.dma_start(
+                out=prec_tiles[unit][:].rearrange("p (j c) -> p j c", j=4),
+                in_=block_view(prec, unit // 2)[:, :, STRIP * (unit % 2) : STRIP * (unit % 2 + 1)],
+            )
 
         def load_c():
             nc.sync.dma_start(
-                out=c_codes[:].bitcast(I32).rearrange("p (g n) -> p g n", g=4),
+                out=c_code_tile[:].bitcast(I32).rearrange("p (g n) -> p g n", g=C_PASSES),
                 in_=c_words.bitcast(I32).rearrange("g p n -> p g n"),
             )
             for q in range(4):
                 nc.sync.dma_start(
-                    out=c_plane[32 * q : 32 * q + 4, :].bitcast(I32).rearrange("r (g n) -> r g n", g=4),
+                    out=c_scale_tile[32 * q : 32 * q + 4, :].bitcast(I32).rearrange("r (g n) -> r g n", g=C_PASSES),
                     in_=c_scales.bitcast(I32)[:, 4 * q : 4 * q + 4, :].rearrange("g r n -> r g n"),
                 )
 
-        def slots(job):
-            kind, i = job
-            if kind == "w":
-                return [((kind, 2 * i + a), g) for g in range(2) for a in range(2)]
-            return [((kind, 2 * i + a), g) for a in range(2) for g in range(2)]
-
-        def load_job(job):
-            for a in range(2):
-                load_rows((job[0], 2 * job[1] + a))
 
         def turn_job(job, half):
-            bank = aux_ps.tile([P, KP], F32, name="aux")
-            for s, (key, g) in enumerate(slots(job)[2 * half : 2 * half + 2]):
-                words = rows[key][:].bitcast(F32)
+            kind, index = job
+            bank = aux_ps.tile([P, BANK], F32, name="aux")
+            for s in range(2):
+                tile_of_job, g = (s, half) if kind == "w" else (half, s)
+                words = rows[(kind, 2 * index + tile_of_job)][:].bitcast(F32)
                 for u in range(2):
                     col = P * (2 * s + u)
-                    nc.tensor.transpose(bank[:, col : col + P], words[:, 256 * g + u : 256 * (g + 1) : 2], ident[:])
-            banks[(job, half)] = bank
+                    nc.tensor.transpose(
+                        bank[:, col : col + P], words[:, PASS_WORDS * g + u : PASS_WORDS * (g + 1) : 2], ident[:]
+                    )
+            turned[(job, half)] = bank
 
-        def pair_copy(eng, dst, bank):
-            out = dst.bitcast(F32).rearrange("p (s m u) -> p s m u", s=2, u=2)
-            copy(eng, out, bank[:].rearrange("p (s u m) -> p s m u", s=2, u=2))
+        def turn_v(block, pair):
+            bank = aux_ps.tile([P, BANK], F32, name="aux")
+            words = v_tiles[block][:].bitcast(F32)
+            for s in range(2):
+                for u in range(2):
+                    src, col = P * (4 * u + 2 * pair + s), P * (2 * s + u)
+                    nc.tensor.transpose(bank[:, col : col + P], words[:, src : src + P], ident[:])
+            turned[("v", block, pair)] = bank
 
-        def copy_job(job, half, eng):
-            if half == 0:
-                stage[job] = flow.tile([P, 4 * KP], BF16, name="stage", bufs=3, align_bytes=64)
-            pair_copy(eng, stage[job][:, 1024 * half : 1024 * (half + 1)], banks[(job, half)])
-
-        def quantise(key, src, width):
-            codes = keep.tile([P, width], U32, name="codes_%s_%d" % key, align_bytes=64)
-            plane = keep.tile([P, width], U8, name="plane_%s_%d" % key, align_bytes=64)
-            nc.vector.quantize_mx(out=codes[:].bitcast(FP8X4), scales=plane[:], in_=src)
-            quant[key] = (codes, plane)
-
-        def operand(key, lo, width):
-            codes, plane = quant[key]
-            return codes[:, lo : lo + width].bitcast(FP8X4), plane[:, lo : lo + width]
-
-        def mx(out, left, right, start, stop):
-            nc.tensor.matmul_mx(
-                out=out, lhsT=left[0], lhsT_scale=left[1], rhs=right[0], rhs_scale=right[1], start=start, stop=stop
+        def join_words(engine, dst, bank):
+            copy(
+                engine,
+                dst.bitcast(F32).rearrange("p (s m u) -> p s m u", s=2, u=2),
+                bank[:].rearrange("p (s u m) -> p s m u", s=2, u=2),
             )
 
-        def synth(n, jp):
-            bank = synth_ps.tile([P, KP], F32, name="synth")
-            for j in range(2):
-                for g in range(2):
-                    left = operand(("y", 2 * (n // 8) + jp), P * (2 * j + g), P)
-                    mx(bank[:, HALF * j : HALF * (j + 1)], left, operand(("w", n % 8), HALF * g, HALF), g == 0, g == 1)
-            acc[(n, jp)] = bank
+        def copy_job(job, half, engine):
+            if half == 0:
+                staged[job] = flow.tile([P, 4 * BANK], BF16, name="job_stage", bufs=3, align_bytes=64)
+            join_words(engine, staged[job][:, 2 * BANK * half : 2 * BANK * (half + 1)], turned[(job, half)])
 
-        def subtract(n, jp):
-            if jp == 0:
-                dt[n] = flow.tile([P, 2 * KP], F32, name="gap", bufs=3)
-            zv = zt[(n // 2, jp)][:].rearrange("p (j c) -> p j c", j=2)
+        def copy_v(block, pair, engine):
+            key = ("v_by_placebo", 2 * block + pair)
+            staged[key] = flow.tile([P, 2 * BANK], BF16, name="v_stage", bufs=3, align_bytes=64)
+            join_words(engine, staged[key][:], turned[("v", block, pair)])
+
+        def quantise(key):
+            columns = staged[key].shape[1] // 4
+            codes = keep.tile([P, columns], U32, name="codes_%s_%d" % key, align_bytes=64)
+            scales = keep.tile([P, columns], U8, name="scales_%s_%d" % key, align_bytes=64)
+            nc.vector.quantize_mx(out=codes[:].bitcast(FP8X4), scales=scales[:], in_=staged[key][:])
+            quantised[key] = (codes, scales)
+
+        def quantise_v(block, pair):
+            quantise(("v_by_placebo", 2 * block + pair))
+
+        def operand(key, first, width):
+            codes, scales = quantised[key]
+            return codes[:, first : first + width].bitcast(FP8X4), scales[:, first : first + width]
+
+        def mx(out, stationary, moving, start, stop):
+            nc.tensor.matmul_mx(
+                out=out,
+                lhsT=stationary[0],
+                lhsT_scale=stationary[1],
+                rhs=moving[0],
+                rhs_scale=moving[1],
+                start=start,
+                stop=stop,
+            )
+
+
+        def synth(unit, pair):
+            bank = synth_ps.tile([P, BANK], F32, name="synth")
+            group, strip = divmod(unit, STRIPS)
+            for s in range(2):
+                for g in range(2):
+                    y_part = operand(("y", 2 * group + pair), P * (2 * s + g), P)
+                    w_part = operand(("w", strip), STRIP * g, STRIP)
+                    mx(bank[:, STRIP * s : STRIP * (s + 1)], y_part, w_part, g == 0, g == 1)
+            synth_banks[(unit, pair)] = bank
+
+        def subtract(unit, pair):
+            if pair == 0:
+                gaps[unit] = flow.tile([P, 2 * BANK], F32, name="gap", bufs=3)
+            z_pair = z_tiles[(unit // 2, pair)][:].rearrange("p (s c) -> p s c", s=2)
             nc.vector.tensor_tensor(
-                out=dt[n][:, KP * jp : KP * (jp + 1)].rearrange("p (j c) -> p j c", j=2),
-                in0=acc[(n, jp)][:].rearrange("p (j c) -> p j c", j=2),
-                in1=zv[:, :, HALF * (n % 2) : HALF * (n % 2 + 1)],
+                out=gaps[unit][:, BANK * pair : BANK * (pair + 1)].rearrange("p (s c) -> p s c", s=2),
+                in0=synth_banks[(unit, pair)][:].rearrange("p (s c) -> p s c", s=2),
+                in1=z_pair[:, :, STRIP * (unit % 2) : STRIP * (unit % 2 + 1)],
                 op=ALU.subtract,
             )
 
-        def square(n, jp):
-            if jp == 0:
-                st[n] = flow.tile([P, 2 * KP], F32, name="sq", bufs=3)
-            cols = slice(KP * jp, KP * (jp + 1))
+        def square(unit, pair):
+            if pair == 0:
+                squares[unit] = flow.tile([P, 2 * BANK], F32, name="square", bufs=3)
+            cols = slice(BANK * pair, BANK * (pair + 1))
             nc.scalar.activation(
-                out=st[n][:, cols].rearrange("p (u c e) -> p u c e", u=2, e=2),
-                in_=dt[n][:, cols].rearrange("p (c u e) -> p u c e", u=2, e=2),
+                out=squares[unit][:, cols].rearrange("p (u c e) -> p u c e", u=2, e=2),
+                in_=gaps[unit][:, cols].rearrange("p (c u e) -> p u c e", u=2, e=2),
                 func=ACT.Square,
             )
 
-        def weigh(n, lo, hi):
-            b, ph = n // 2, n % 2
-            if b not in xt:
-                xt[b] = flow.tile([P, 4 * KP], BF16, name="v", bufs=3)
-            cols = slice(64 * ph, 64 * (ph + 1))
+        def weigh(unit):
+            block, half = divmod(unit, 2)
+            if half == 0:
+                v_tiles[block] = flow.tile([P, 4 * PASS], BF16, name="v", bufs=3)
+            v_view = v_tiles[block][:].rearrange("p (u q s m e) -> p u q s m e", u=2, q=2, s=2, e=2)
             nc.vector.tensor_tensor(
-                out=xt[b][:].rearrange("p (u q j m e) -> p u q j m e", u=2, q=2, j=2, e=2)[:, :, lo:hi, :, cols],
-                in0=st[n][:].rearrange("p (q u j m e) -> p u q j m e", u=2, q=2, j=2, e=2)[:, :, lo:hi],
-                in1=pt[n][:].rearrange("p (q j m u e) -> p u q j m e", u=2, q=2, j=2, e=2)[:, :, lo:hi],
+                out=v_view[:, :, :, :, 64 * half : 64 * (half + 1)],
+                in0=squares[unit][:].rearrange("p (q u s m e) -> p u q s m e", u=2, q=2, s=2, e=2),
+                in1=prec_tiles[unit][:].rearrange("p (q s m u e) -> p u q s m e", u=2, q=2, s=2, e=2),
                 op=ALU.mult,
             )
 
-        def turn_v(b, jp):
-            bank = aux_ps.tile([P, KP], F32, name="aux")
-            words = xt[b][:].bitcast(F32)
-            for s in range(2):
-                for u in range(2):
-                    src = P * (4 * u + 2 * jp + s)
-                    nc.tensor.transpose(bank[:, P * (2 * s + u) : P * (2 * s + u + 1)], words[:, src : src + P], ident[:])
-            banks[("v", b, jp)] = bank
-
-        def copy_v(b, jp, eng):
-            stage[("v", b, jp)] = flow.tile([P, 2 * KP], BF16, name="vstage", bufs=3, align_bytes=64)
-            pair_copy(eng, stage[("v", b, jp)][:], banks[("v", b, jp)])
-
-        def quantise_v(b, jp):
-            quantise(("vt", 2 * b + jp), stage[("v", b, jp)][:], HALF)
-
-        def interleave(n, eng, u):
-            k, gt = n % 8, n // 8
-            if k not in astage:
-                astage[k] = flow.tile([P, 4 * KP], BF16, name="astage", bufs=8, align_bytes=64)
-            if eng == "G":
-                src = xt[n // 2][:].rearrange("p (u j h c) -> p h u c j", u=2, j=4, h=2)[:, n % 2, u]
-                dst = astage[k][:].rearrange("p (g u c j) -> p g u c j", g=2, u=2, j=4)[:, gt, u]
-                nc.gpsimd.tensor_scalar(out=dst, in0=src, scalar1=1.0, scalar2=0.0, op0=ALU.mult, op1=ALU.add)
-            else:
-                src = xt[n // 2][:].rearrange("p (u j h c i) -> p h u c j i", u=2, j=4, h=2, i=4)[:, n % 2, u]
-                dst = astage[k][:].rearrange("p (g u c i j) -> p g u c j i", g=2, u=2, i=4, j=4)[:, gt, u]
-                copy(eng, dst, src)
-
-        def unit_passes(gt, j, pool, name, first, last):
-            if first == 0:
-                outs[("unit", gt, j)] = pool.tile([P, KP], F32, name=name)
-            for pb in range(first, last):
-                rhs = (c_codes[:, 2 * G * pb : 2 * G * (pb + 1)].bitcast(FP4X4), c_plane[:, G * pb : G * (pb + 1)])
-                left = operand(("vt", 8 * gt + 2 * pb + j // 2), P * (j % 2), P)
-                mx(outs[("unit", gt, j)][:], left, rhs, pb == 0, pb == 3)
-
-        def time_passes(k, ap):
-            bank = aux_ps.tile([P, KP], F32, name="aux")
-            for a in range(2):
-                for gt in range(2):
-                    left = operand(("win", ap), P * (2 * a + gt), P)
-                    mx(bank[:, HALF * a : HALF * (a + 1)], left, operand(("v", k), HALF * gt, HALF), gt == 0, gt == 1)
-            outs[("time", k, ap)] = bank
-
-        def emit(key, eng):
-            kind, grp, i = key
-            res = flow.tile([P, KP], F32, name="res", bufs=8)
-            if kind == "unit":
-                copy(eng, res[:], outs[key][:])
-                dest = out_0[KP * grp : KP * (grp + 1), :].rearrange("(m j) n -> m j n", j=4)[:, i, :]
-                nc.sync.dma_start(out=dest, in_=res[:])
-            else:
-                copy(
-                    eng,
-                    res[:].rearrange("p (a c u e) -> p a c u e", a=2, u=2, e=2),
-                    outs[key][:].rearrange("p (a u c e) -> p a c u e", a=2, u=2, e=2),
+        def interleave(unit, u, engine):
+            group, strip = divmod(unit, STRIPS)
+            block, half = divmod(unit, 2)
+            key = ("v_by_period", strip)
+            if key not in staged:
+                staged[key] = flow.tile([P, 2 * 4 * STRIP], BF16, name="strip_stage", bufs=STRIPS, align_bytes=64)
+            if engine == GPSIMD:
+                src = v_tiles[block][:].rearrange("p (u j h c) -> p h u c j", u=2, j=4, h=2)
+                dst = staged[key][:].rearrange("p (g u c j) -> p g u c j", g=2, u=2, j=4)
+                nc.gpsimd.tensor_scalar(
+                    out=dst[:, group, u], in0=src[:, half, u], scalar1=1.0, scalar2=0.0, op0=ALU.mult, op1=ALU.add
                 )
-                dest = out_1.rearrange("(m a) n -> m a n", a=4)[:, 2 * i : 2 * i + 2, HALF * grp : HALF * (grp + 1)]
-                nc.sync.dma_start(out=dest, in_=res[:].rearrange("p (a c) -> p a c", a=2))
+            else:
+                src = v_tiles[block][:].rearrange("p (u j h c i) -> p h u c j i", u=2, j=4, h=2, i=4)
+                dst = staged[key][:].rearrange("p (g u c i j) -> p g u c j i", g=2, u=2, i=4, j=4)
+                copy(engine, dst[:, group, u], src[:, half, u])
 
-        later_jobs = [("w", i) for i in range(3, 8)] + [("y", 2), ("y", 3), ("win", 0), ("win", 1)]
 
-        def loads(need):
-            if need % 2 == 0 and 0 < need < UNITS:
-                load_z(need // 2, 0)
-                load_z(need // 2, 1)
-            if 0 < need <= UNITS:
-                load_prec(need - 1)
-            if need < len(later_jobs):
-                load_job(later_jobs[need])
-            if need == 9:
+        def unit_passes(group, slot, first, last):
+            if first == 0:
+                pool, name = (aux_ps, "aux") if group == 0 else (synth_ps, "synth")
+                results[("unit", group, slot)] = pool.tile([P, BANK], F32, name=name)
+            for g in range(first, last):
+                v_part = operand(("v_by_placebo", 2 * (C_PASSES * group + g) + slot // 2), P * (slot % 2), P)
+                c_part = (
+                    c_code_tile[:, 2 * UNIT_CONTRASTS * g : 2 * UNIT_CONTRASTS * (g + 1)].bitcast(FP4X4),
+                    c_scale_tile[:, UNIT_CONTRASTS * g : UNIT_CONTRASTS * (g + 1)],
+                )
+                mx(results[("unit", group, slot)][:], v_part, c_part, g == 0, g == C_PASSES - 1)
+
+        def time_passes(strip, win_job):
+            bank = aux_ps.tile([P, BANK], F32, name="aux")
+            for s in range(2):
+                for group in range(2):
+                    win_part = operand(("win", win_job), P * (2 * s + group), P)
+                    v_part = operand(("v_by_period", strip), STRIP * group, STRIP)
+                    mx(bank[:, STRIP * s : STRIP * (s + 1)], win_part, v_part, group == 0, group == 1)
+            results[("time", strip, win_job)] = bank
+
+        def result_tile():
+            return flow.tile([P, BANK], F32, name="result", bufs=8)
+
+        def store_unit(group, slot, engine):
+            res = result_tile()
+            copy(engine, res[:], results[("unit", group, slot)][:])
+            periods = out_0[PASS * group : PASS * (group + 1), :].rearrange("(m j) n -> m j n", j=4)
+            nc.sync.dma_start(out=periods[:, slot, :], in_=res[:])
+
+        def store_time(strip, win_job, engine):
+            res = result_tile()
+            copy(
+                engine,
+                res[:].rearrange("p (s m u e) -> p s m u e", s=2, u=2, e=2),
+                results[("time", strip, win_job)][:].rearrange("p (s u m e) -> p s m u e", s=2, u=2, e=2),
+            )
+            contrasts = out_1.rearrange("(m j) n -> m j n", j=4)
+            nc.sync.dma_start(
+                out=contrasts[:, 2 * win_job : 2 * win_job + 2, STRIP * strip : STRIP * (strip + 1)],
+                in_=res[:].rearrange("p (s c) -> p s c", s=2),
+            )
+
+
+        step_jobs = [("w", strip) for strip in range(3, STRIPS)] + [("y", 2), ("y", 3), ("win", 0), ("win", 1)]
+        first_steps = len(step_jobs)
+        first_unit_step = first_steps + 1
+
+        def loads(step):
+            if step % 2 == 0 and 0 < step < UNITS:
+                load_z(step // 2, 0)
+                load_z(step // 2, 1)
+            if 0 < step <= UNITS:
+                load_prec(step - 1)
+            if step < first_steps:
+                load_job(step_jobs[step])
+            if step == first_unit_step - 1:
                 load_c()
 
         load_job(("y", 0))
@@ -250,137 +292,136 @@ def tile_synthetic_control_placebos_s8_kernel(tc, y, w, z, prec, c_words, c_scal
         load_z(0, 1)
         load_job(("w", 2))
         for job in (("y", 0), ("w", 0)):
-            for half in range(2):
+            for half, engine in enumerate((VECTOR, SCALAR)):
                 turn_job(job, half)
-                copy_job(job, half, "SV"[half])
-            quantise(job, stage[job][:], KP)
+                copy_job(job, half, engine)
+            quantise(job)
         for half in range(2):
             turn_job(("y", 1), half)
-            copy_job(("y", 1), half, "S")
-        for need in range(LEAD):
-            loads(need)
+            copy_job(("y", 1), half, SCALAR)
+        for step in range(LEAD):
+            loads(step)
         synth(0, 0)
-        quantise(("y", 1), stage[("y", 1)][:], KP)
+        quantise(("y", 1))
         for half in range(2):
             turn_job(("w", 1), half)
-        copy_job(("w", 1), 0, "S")
+        copy_job(("w", 1), 0, SCALAR)
         synth(0, 1)
         subtract(0, 0)
-        copy_job(("w", 1), 1, "V")
+        copy_job(("w", 1), 1, VECTOR)
         square(0, 0)
         for half in range(2):
             turn_job(("w", 2), half)
         subtract(0, 1)
-        quantise(("w", 1), stage[("w", 1)][:], KP)
-        copy_job(("w", 2), 0, "S")
-        copy_job(("w", 2), 1, "V")
-        pending = ("w", 2)
+        quantise(("w", 1))
+        copy_job(("w", 2), 0, VECTOR)
+        copy_job(("w", 2), 1, SCALAR)
 
-        for n in range(9):
+        for n in range(first_steps):
             loads(n + LEAD)
-            job = later_jobs[n]
+            job = step_jobs[n]
             turn_job(job, 0)
             if n >= 2:
-                interleave(n - 2, "S", 0)
+                interleave(n - 2, 0, SCALAR)
             if n > 0:
                 subtract(n, 0)
                 square(n, 0)
                 subtract(n, 1)
-            if n >= 4 and n % 2 == 1:
-                copy_v(*divmod(n - 4, 2), "V")
-            quantise(pending, stage[pending][:], KP)
-            pending = job
+            quantise(step_jobs[n - 1] if n > 0 else ("w", 2))
             turn_job(job, 1)
             if n >= 3:
                 turn_v(*divmod(n - 3, 2))
             synth(n + 1, 0)
             synth(n + 1, 1)
             square(n, 1)
-            copy_job(job, 0, "S")
-            copy_job(job, 1, "S")
+            copy_job(job, 0, SCALAR)
+            copy_job(job, 1, SCALAR)
             if n >= 4:
                 quantise_v(*divmod(n - 4, 2))
-            if n >= 3 and n % 2 == 1:
-                copy_v(*divmod(n - 3, 2), "S")
+            if n >= 3:
+                copy_v(*divmod(n - 3, 2), SCALAR)
             if n >= 1:
-                weigh(n - 1, 0, 2)
-                interleave(n - 1, "G", 1)
-        turn_v(3, 0)
-        interleave(7, "S", 0)
-        copy_v(2, 1, "S")
-        copy_v(3, 0, "S")
-        weigh(8, 0, 2)
-        interleave(8, "G", 1)
+                weigh(n - 1)
+                interleave(n - 1, 1, GPSIMD if n + 1 < first_steps else SCALAR)
 
-        for n in range(9, UNITS):
+        last_block = C_PASSES - 1
+        turn_v(last_block, 0)
+        interleave(first_steps - 2, 0, SCALAR)
+        copy_v(last_block, 0, SCALAR)
+        weigh(first_steps - 1)
+        interleave(first_steps - 1, 1, GPSIMD)
+
+        for n in range(first_steps, UNITS):
+            ready_strip = n - first_steps - 1
+            unit_slot = n - first_unit_step
+            last_step = n + 1 == UNITS
             loads(n + LEAD)
-            if n + 1 < UNITS:
-                synth(n + 1, 0)
-                synth(n + 1, 1)
+            for i in range(2):
+                if last_step:
+                    unit_passes(1, i, 0, 2)
+                else:
+                    synth(n + 1, i)
+            if ready_strip >= 0:
+                time_passes(ready_strip, 0)
+                time_passes(ready_strip, 1)
+            interleave(n - 1, 0, SCALAR)
+            for pair in range(2):
+                subtract(n, pair)
+                square(n, pair)
+            if 1 <= unit_slot <= 4:
+                store_unit(0, unit_slot - 1, SCALAR if n % 2 else VECTOR)
+            if n == first_steps:
+                quantise(step_jobs[-1])
+                quantise_v(last_block - 1, 1)
+                quantise_v(last_block, 0)
             else:
-                for j in range(2):
-                    unit_passes(1, j, synth_ps, "synth", 0, 2)
-            if n > 9:
-                time_passes(n - 10, 0)
-                time_passes(n - 10, 1)
-            interleave(n - 1, "S", 0)
-            subtract(n, 0)
-            square(n, 0)
-            subtract(n, 1)
-            square(n, 1)
-            if 11 <= n < 15:
-                emit(("unit", 0, n - 11), "V")
-            if n == 9:
-                quantise(pending, stage[pending][:], KP)
-                quantise_v(2, 1)
-                quantise_v(3, 0)
-            if n >= 10:
-                copy_v(*divmod(n - 3, 2), "S")
-            if n >= 11:
+                copy_v(*divmod(n - 3, 2), SCALAR)
+            if n >= first_steps + 2:
                 quantise_v(*divmod(n - 4, 2))
-            if 10 <= n < 14:
-                unit_passes(0, n - 10, aux_ps, "aux", 0, 4)
-            if n == 15:
-                for j in (2, 3):
-                    unit_passes(1, j, synth_ps, "synth", 0, 2)
-            if n > 9:
-                emit(("time", n - 10, 0), "S")
+            if 0 <= unit_slot < 4:
+                unit_passes(0, unit_slot, 0, C_PASSES)
+            if last_step:
+                for slot in (2, 3):
+                    unit_passes(1, slot, 0, 2)
+            if ready_strip >= 0:
+                store_time(ready_strip, 0, SCALAR)
             turn_v(*divmod(n - 2, 2))
-            quantise(("v", n - 9), astage[n - 9][:], KP)
-            if n > 9:
-                emit(("time", n - 10, 1), "S")
-            if n + 1 < UNITS:
-                weigh(n, 0, 2)
-                interleave(n, "G", 1)
+            quantise(("v_by_period", ready_strip + 1))
+            if ready_strip >= 0:
+                store_time(ready_strip, 1, SCALAR)
+            if not last_step:
+                weigh(n)
+                interleave(n, 1, GPSIMD)
 
-        time_passes(6, 0)
-        copy_v(6, 1, "S")
-        weigh(15, 0, 2)
-        turn_v(7, 0)
-        turn_v(7, 1)
-        quantise_v(6, 0)
-        interleave(15, "V", 1)
-        copy_v(7, 0, "S")
-        interleave(15, "V", 0)
-        for j in range(2):
-            unit_passes(1, j, synth_ps, "synth", 2, 3)
-        time_passes(6, 1)
-        emit(("time", 6, 0), "S")
-        quantise_v(6, 1)
-        quantise_v(7, 0)
-        for j in range(2):
-            unit_passes(1, j, synth_ps, "synth", 3, 4)
-        quantise(("v", 7), astage[7][:], KP)
-        emit(("time", 6, 1), "S")
-        copy_v(7, 1, "V")
-        time_passes(7, 0)
-        time_passes(7, 1)
-        emit(("unit", 1, 0), "S")
-        emit(("unit", 1, 1), "V")
-        quantise_v(7, 1)
-        for j in (2, 3):
-            unit_passes(1, j, synth_ps, "synth", 2, 4)
-        emit(("time", 7, 0), "S")
-        emit(("time", 7, 1), "V")
-        emit(("unit", 1, 2), "S")
-        emit(("unit", 1, 3), "V")
+        end_block, end_strip, end_unit = UNITS // 2 - 1, STRIPS - 1, UNITS - 1
+        time_passes(end_strip - 1, 0)
+        copy_v(end_block - 1, 1, SCALAR)
+        weigh(end_unit)
+        turn_v(end_block, 0)
+        turn_v(end_block, 1)
+        quantise_v(end_block - 1, 0)
+        interleave(end_unit, 1, VECTOR)
+        copy_v(end_block, 0, SCALAR)
+        interleave(end_unit, 0, VECTOR)
+        for slot in (0, 1):
+            unit_passes(1, slot, 2, 3)
+        time_passes(end_strip - 1, 1)
+        store_time(end_strip - 1, 0, SCALAR)
+        quantise_v(end_block - 1, 1)
+        quantise_v(end_block, 0)
+        for slot in (0, 1):
+            unit_passes(1, slot, 3, C_PASSES)
+        quantise(("v_by_period", end_strip))
+        store_time(end_strip - 1, 1, SCALAR)
+        copy_v(end_block, 1, VECTOR)
+        time_passes(end_strip, 0)
+        time_passes(end_strip, 1)
+        store_unit(1, 0, SCALAR)
+        store_unit(1, 1, VECTOR)
+        quantise_v(end_block, 1)
+        for slot in (2, 3):
+            unit_passes(1, slot, 2, C_PASSES)
+        store_time(end_strip, 0, SCALAR)
+        store_time(end_strip, 1, VECTOR)
+        store_unit(1, 2, SCALAR)
+        store_unit(1, 3, VECTOR)

from contextlib import ExitStack

import concourse.mybir as mybir
from concourse.masks import make_identity

PERIODS, DONORS, PLACEBOS, UNIT_CONTRASTS, TIME_CONTRASTS = 1024, 1024, 2048, 512, 512
FLOPS = 2 * PERIODS * PLACEBOS * (DONORS + UNIT_CONTRASTS + TIME_CONTRASTS)

F32 = mybir.dt.float32
BF16 = mybir.dt.bfloat16
U32 = mybir.dt.uint32
I32 = mybir.dt.int32
U8 = mybir.dt.uint8
FP8X4 = mybir.dt.float8_e4m3fn_x4
FP4X4 = mybir.dt.float4_e2m1fn_x4
ALU = mybir.AluOpType
ACT = mybir.ActivationFunctionType
ENGINE = mybir.EngineType

P = 128
PASS = 512
BANK = 512
STRIP = 256
PASS_WORDS = PASS // 2
UNITS = 16
STRIPS = 8
C_PASSES = PLACEBOS // PASS
LEAD = 3
VECTOR, SCALAR, GPSIMD = "vector", "scalar", "gpsimd"


def tile_synthetic_control_placebos_s8_kernel(tc, y, w, z, prec, c_words, c_scales, win, out_0, out_1):
    nc = tc.nc
    with ExitStack() as ctx:
        keep = ctx.enter_context(tc.tile_pool(name="keep", bufs=1))
        flow = ctx.enter_context(tc.tile_pool(name="flow", bufs=2))
        synth_ps = ctx.enter_context(tc.psum_pool(name="synth_ps", bufs=4))
        aux_ps = ctx.enter_context(tc.psum_pool(name="aux_ps", bufs=4))
        ctx.enter_context(tc.manual_schedule(engines={ENGINE.SP, ENGINE.PE, ENGINE.DVE, ENGINE.Pool}))

        ident_root = keep.tile([P, P], F32, name="ident_root")
        make_identity(nc, ident_root[:])
        ident = keep.tile([P, P], F32, name="ident")
        nc.scalar.activation(out=ident[:], in_=ident_root[:], func=ACT.Square)
        c_scale_tile = keep.tile([P, C_PASSES * UNIT_CONTRASTS], U8, name="c_scale_tile", align_bytes=64)
        nc.gpsimd.memset(c_scale_tile[:].bitcast(U32), 0)
        c_code_tile = keep.tile([P, C_PASSES * 2 * UNIT_CONTRASTS], U8, name="c_code_tile", align_bytes=64)

        rows, z_tiles, prec_tiles = {}, {}, {}
        synth_banks, gaps, squares, v_tiles = {}, {}, {}, {}
        turned, staged, quantised, results = {}, {}, {}, {}

        def copy(engine, out, src):
            if engine == SCALAR:
                nc.scalar.copy(out=out, in_=src)
            else:
                nc.vector.tensor_copy(out=out, in_=src)


        def load_job(job):
            kind, index = job
            for i in (2 * index, 2 * index + 1):
                if kind == "w":
                    src = w[P * i : P * (i + 1), :]
                else:
                    run = (y if kind == "y" else win)[PASS * (i // 4) : PASS * (i // 4 + 1), :]
                    src = run.rearrange("(m j) k -> m j k", j=4)[:, i % 4, :]
                rows[(kind, i)] = flow.tile([P, DONORS], BF16, name="rows", bufs=10)
                nc.sync.dma_start(out=rows[(kind, i)][:], in_=src)

        def block_view(src, block):
            group, c_pass = divmod(block, C_PASSES)
            cells = src[PASS * group : PASS * (group + 1), PASS * c_pass : PASS * (c_pass + 1)]
            return cells.rearrange("(m j) c -> m j c", j=4)

        def load_z(block, pair):
            z_tiles[(block, pair)] = flow.tile([P, 2 * PASS], BF16, name="z_tile", bufs=6)
            nc.sync.dma_start(
                out=z_tiles[(block, pair)][:].rearrange("p (j c) -> p j c", j=2),
                in_=block_view(z, block)[:, 2 * pair : 2 * pair + 2, :],
            )

        def load_prec(unit):
            prec_tiles[unit] = flow.tile([P, 4 * STRIP], BF16, name="prec_tile", bufs=6)
            nc.sync.dma_start(
                out=prec_tiles[unit][:].rearrange("p (j c) -> p j c", j=4),
                in_=block_view(prec, unit // 2)[:, :, STRIP * (unit % 2) : STRIP * (unit % 2 + 1)],
            )

        def load_c():
            nc.sync.dma_start(
                out=c_code_tile[:].bitcast(I32).rearrange("p (g n) -> p g n", g=C_PASSES),
                in_=c_words.bitcast(I32).rearrange("g p n -> p g n"),
            )
            for q in range(4):
                nc.sync.dma_start(
                    out=c_scale_tile[32 * q : 32 * q + 4, :].bitcast(I32).rearrange("r (g n) -> r g n", g=C_PASSES),
                    in_=c_scales.bitcast(I32)[:, 4 * q : 4 * q + 4, :].rearrange("g r n -> r g n"),
                )


        def turn_job(job, half):
            kind, index = job
            bank = aux_ps.tile([P, BANK], F32, name="aux")
            for s in range(2):
                tile_of_job, g = (s, half) if kind == "w" else (half, s)
                words = rows[(kind, 2 * index + tile_of_job)][:].bitcast(F32)
                for u in range(2):
                    col = P * (2 * s + u)
                    nc.tensor.transpose(
                        bank[:, col : col + P], words[:, PASS_WORDS * g + u : PASS_WORDS * (g + 1) : 2], ident[:]
                    )
            turned[(job, half)] = bank

        def turn_v(block, pair):
            bank = aux_ps.tile([P, BANK], F32, name="aux")
            words = v_tiles[block][:].bitcast(F32)
            for s in range(2):
                for u in range(2):
                    src, col = P * (4 * u + 2 * pair + s), P * (2 * s + u)
                    nc.tensor.transpose(bank[:, col : col + P], words[:, src : src + P], ident[:])
            turned[("v", block, pair)] = bank

        def join_words(engine, dst, bank):
            copy(
                engine,
                dst.bitcast(F32).rearrange("p (s m u) -> p s m u", s=2, u=2),
                bank[:].rearrange("p (s u m) -> p s m u", s=2, u=2),
            )

        def copy_job(job, half, engine):
            if half == 0:
                staged[job] = flow.tile([P, 4 * BANK], BF16, name="job_stage", bufs=3, align_bytes=64)
            join_words(engine, staged[job][:, 2 * BANK * half : 2 * BANK * (half + 1)], turned[(job, half)])

        def copy_v(block, pair, engine):
            key = ("v_by_placebo", 2 * block + pair)
            staged[key] = flow.tile([P, 2 * BANK], BF16, name="v_stage", bufs=3, align_bytes=64)
            join_words(engine, staged[key][:], turned[("v", block, pair)])

        def quantise(key):
            columns = staged[key].shape[1] // 4
            codes = keep.tile([P, columns], U32, name="codes_%s_%d" % key, align_bytes=64)
            scales = keep.tile([P, columns], U8, name="scales_%s_%d" % key, align_bytes=64)
            nc.vector.quantize_mx(out=codes[:].bitcast(FP8X4), scales=scales[:], in_=staged[key][:])
            quantised[key] = (codes, scales)

        def quantise_v(block, pair):
            quantise(("v_by_placebo", 2 * block + pair))

        def operand(key, first, width):
            codes, scales = quantised[key]
            return codes[:, first : first + width].bitcast(FP8X4), scales[:, first : first + width]

        def mx(out, stationary, moving, start, stop):
            nc.tensor.matmul_mx(
                out=out,
                lhsT=stationary[0],
                lhsT_scale=stationary[1],
                rhs=moving[0],
                rhs_scale=moving[1],
                start=start,
                stop=stop,
            )


        def synth(unit, pair):
            bank = synth_ps.tile([P, BANK], F32, name="synth")
            group, strip = divmod(unit, STRIPS)
            for s in range(2):
                for g in range(2):
                    y_part = operand(("y", 2 * group + pair), P * (2 * s + g), P)
                    w_part = operand(("w", strip), STRIP * g, STRIP)
                    mx(bank[:, STRIP * s : STRIP * (s + 1)], y_part, w_part, g == 0, g == 1)
            synth_banks[(unit, pair)] = bank

        def subtract(unit, pair):
            if pair == 0:
                gaps[unit] = flow.tile([P, 2 * BANK], F32, name="gap", bufs=3)
            z_pair = z_tiles[(unit // 2, pair)][:].rearrange("p (s c) -> p s c", s=2)
            nc.vector.tensor_tensor(
                out=gaps[unit][:, BANK * pair : BANK * (pair + 1)].rearrange("p (s c) -> p s c", s=2),
                in0=synth_banks[(unit, pair)][:].rearrange("p (s c) -> p s c", s=2),
                in1=z_pair[:, :, STRIP * (unit % 2) : STRIP * (unit % 2 + 1)],
                op=ALU.subtract,
            )

        def square(unit, pair):
            if pair == 0:
                squares[unit] = flow.tile([P, 2 * BANK], F32, name="square", bufs=3)
            cols = slice(BANK * pair, BANK * (pair + 1))
            nc.scalar.activation(
                out=squares[unit][:, cols].rearrange("p (u c e) -> p u c e", u=2, e=2),
                in_=gaps[unit][:, cols].rearrange("p (c u e) -> p u c e", u=2, e=2),
                func=ACT.Square,
            )

        def weigh(unit):
            block, half = divmod(unit, 2)
            if half == 0:
                v_tiles[block] = flow.tile([P, 4 * PASS], BF16, name="v", bufs=3)
            v_view = v_tiles[block][:].rearrange("p (u q s m e) -> p u q s m e", u=2, q=2, s=2, e=2)
            nc.vector.tensor_tensor(
                out=v_view[:, :, :, :, 64 * half : 64 * (half + 1)],
                in0=squares[unit][:].rearrange("p (q u s m e) -> p u q s m e", u=2, q=2, s=2, e=2),
                in1=prec_tiles[unit][:].rearrange("p (q s m u e) -> p u q s m e", u=2, q=2, s=2, e=2),
                op=ALU.mult,
            )

        def interleave(unit, u, engine):
            group, strip = divmod(unit, STRIPS)
            block, half = divmod(unit, 2)
            key = ("v_by_period", strip)
            if key not in staged:
                staged[key] = flow.tile([P, 2 * 4 * STRIP], BF16, name="strip_stage", bufs=STRIPS, align_bytes=64)
            if engine == GPSIMD:
                src = v_tiles[block][:].rearrange("p (u j h c) -> p h u c j", u=2, j=4, h=2)
                dst = staged[key][:].rearrange("p (g u c j) -> p g u c j", g=2, u=2, j=4)
                nc.gpsimd.tensor_scalar(
                    out=dst[:, group, u], in0=src[:, half, u], scalar1=1.0, scalar2=0.0, op0=ALU.mult, op1=ALU.add
                )
            else:
                src = v_tiles[block][:].rearrange("p (u j h c i) -> p h u c j i", u=2, j=4, h=2, i=4)
                dst = staged[key][:].rearrange("p (g u c i j) -> p g u c j i", g=2, u=2, i=4, j=4)
                copy(engine, dst[:, group, u], src[:, half, u])


        def unit_passes(group, slot, first, last):
            if first == 0:
                pool, name = (aux_ps, "aux") if group == 0 else (synth_ps, "synth")
                results[("unit", group, slot)] = pool.tile([P, BANK], F32, name=name)
            for g in range(first, last):
                v_part = operand(("v_by_placebo", 2 * (C_PASSES * group + g) + slot // 2), P * (slot % 2), P)
                c_part = (
                    c_code_tile[:, 2 * UNIT_CONTRASTS * g : 2 * UNIT_CONTRASTS * (g + 1)].bitcast(FP4X4),
                    c_scale_tile[:, UNIT_CONTRASTS * g : UNIT_CONTRASTS * (g + 1)],
                )
                mx(results[("unit", group, slot)][:], v_part, c_part, g == 0, g == C_PASSES - 1)

        def time_passes(strip, win_job):
            bank = aux_ps.tile([P, BANK], F32, name="aux")
            for s in range(2):
                for group in range(2):
                    win_part = operand(("win", win_job), P * (2 * s + group), P)
                    v_part = operand(("v_by_period", strip), STRIP * group, STRIP)
                    mx(bank[:, STRIP * s : STRIP * (s + 1)], win_part, v_part, group == 0, group == 1)
            results[("time", strip, win_job)] = bank

        def result_tile():
            return flow.tile([P, BANK], F32, name="result", bufs=8)

        def store_unit(group, slot, engine):
            res = result_tile()
            copy(engine, res[:], results[("unit", group, slot)][:])
            periods = out_0[PASS * group : PASS * (group + 1), :].rearrange("(m j) n -> m j n", j=4)
            nc.sync.dma_start(out=periods[:, slot, :], in_=res[:])

        def store_time(strip, win_job, engine):
            res = result_tile()
            copy(
                engine,
                res[:].rearrange("p (s m u e) -> p s m u e", s=2, u=2, e=2),
                results[("time", strip, win_job)][:].rearrange("p (s u m e) -> p s m u e", s=2, u=2, e=2),
            )
            contrasts = out_1.rearrange("(m j) n -> m j n", j=4)
            nc.sync.dma_start(
                out=contrasts[:, 2 * win_job : 2 * win_job + 2, STRIP * strip : STRIP * (strip + 1)],
                in_=res[:].rearrange("p (s c) -> p s c", s=2),
            )


        step_jobs = [("w", strip) for strip in range(3, STRIPS)] + [("y", 2), ("y", 3), ("win", 0), ("win", 1)]
        first_steps = len(step_jobs)
        first_unit_step = first_steps + 1

        def loads(step):
            if step % 2 == 0 and 0 < step < UNITS:
                load_z(step // 2, 0)
                load_z(step // 2, 1)
            if 0 < step <= UNITS:
                load_prec(step - 1)
            if step < first_steps:
                load_job(step_jobs[step])
            if step == first_unit_step - 1:
                load_c()

        load_job(("y", 0))
        load_job(("w", 0))
        load_job(("y", 1))
        load_z(0, 0)
        load_job(("w", 1))
        load_z(0, 1)
        load_job(("w", 2))
        for job in (("y", 0), ("w", 0)):
            for half, engine in enumerate((VECTOR, SCALAR)):
                turn_job(job, half)
                copy_job(job, half, engine)
            quantise(job)
        for half in range(2):
            turn_job(("y", 1), half)
            copy_job(("y", 1), half, SCALAR)
        for step in range(LEAD):
            loads(step)
        synth(0, 0)
        quantise(("y", 1))
        for half in range(2):
            turn_job(("w", 1), half)
        copy_job(("w", 1), 0, SCALAR)
        synth(0, 1)
        subtract(0, 0)
        copy_job(("w", 1), 1, VECTOR)
        square(0, 0)
        for half in range(2):
            turn_job(("w", 2), half)
        subtract(0, 1)
        quantise(("w", 1))
        copy_job(("w", 2), 0, VECTOR)
        copy_job(("w", 2), 1, SCALAR)

        for n in range(first_steps):
            loads(n + LEAD)
            job = step_jobs[n]
            turn_job(job, 0)
            if n >= 2:
                interleave(n - 2, 0, SCALAR)
            if n > 0:
                subtract(n, 0)
                square(n, 0)
                subtract(n, 1)
            quantise(step_jobs[n - 1] if n > 0 else ("w", 2))
            turn_job(job, 1)
            if n >= 3:
                turn_v(*divmod(n - 3, 2))
            synth(n + 1, 0)
            synth(n + 1, 1)
            square(n, 1)
            copy_job(job, 0, SCALAR)
            copy_job(job, 1, SCALAR)
            if n >= 4:
                quantise_v(*divmod(n - 4, 2))
            if n >= 3:
                copy_v(*divmod(n - 3, 2), SCALAR)
            if n >= 1:
                weigh(n - 1)
                interleave(n - 1, 1, GPSIMD if n + 1 < first_steps else SCALAR)

        last_block = C_PASSES - 1
        turn_v(last_block, 0)
        interleave(first_steps - 2, 0, SCALAR)
        copy_v(last_block, 0, SCALAR)
        weigh(first_steps - 1)
        interleave(first_steps - 1, 1, GPSIMD)

        for n in range(first_steps, UNITS):
            ready_strip = n - first_steps - 1
            unit_slot = n - first_unit_step
            last_step = n + 1 == UNITS
            loads(n + LEAD)
            for i in range(2):
                if last_step:
                    unit_passes(1, i, 0, 2)
                else:
                    synth(n + 1, i)
            if ready_strip >= 0:
                time_passes(ready_strip, 0)
                time_passes(ready_strip, 1)
            interleave(n - 1, 0, SCALAR)
            for pair in range(2):
                subtract(n, pair)
                square(n, pair)
            if 1 <= unit_slot <= 4:
                store_unit(0, unit_slot - 1, SCALAR if n % 2 else VECTOR)
            if n == first_steps:
                quantise(step_jobs[-1])
                quantise_v(last_block - 1, 1)
                quantise_v(last_block, 0)
            else:
                copy_v(*divmod(n - 3, 2), SCALAR)
            if n >= first_steps + 2:
                quantise_v(*divmod(n - 4, 2))
            if 0 <= unit_slot < 4:
                unit_passes(0, unit_slot, 0, C_PASSES)
            if last_step:
                for slot in (2, 3):
                    unit_passes(1, slot, 0, 2)
            if ready_strip >= 0:
                store_time(ready_strip, 0, SCALAR)
            turn_v(*divmod(n - 2, 2))
            quantise(("v_by_period", ready_strip + 1))
            if ready_strip >= 0:
                store_time(ready_strip, 1, SCALAR)
            if not last_step:
                weigh(n)
                interleave(n, 1, GPSIMD)

        end_block, end_strip, end_unit = UNITS // 2 - 1, STRIPS - 1, UNITS - 1
        time_passes(end_strip - 1, 0)
        copy_v(end_block - 1, 1, SCALAR)
        weigh(end_unit)
        turn_v(end_block, 0)
        turn_v(end_block, 1)
        quantise_v(end_block - 1, 0)
        interleave(end_unit, 1, VECTOR)
        copy_v(end_block, 0, SCALAR)
        interleave(end_unit, 0, VECTOR)
        for slot in (0, 1):
            unit_passes(1, slot, 2, 3)
        time_passes(end_strip - 1, 1)
        store_time(end_strip - 1, 0, SCALAR)
        quantise_v(end_block - 1, 1)
        quantise_v(end_block, 0)
        for slot in (0, 1):
            unit_passes(1, slot, 3, C_PASSES)
        quantise(("v_by_period", end_strip))
        store_time(end_strip - 1, 1, SCALAR)
        copy_v(end_block, 1, VECTOR)
        time_passes(end_strip, 0)
        time_passes(end_strip, 1)
        store_unit(1, 0, SCALAR)
        store_unit(1, 1, VECTOR)
        quantise_v(end_block, 1)
        for slot in (2, 3):
            unit_passes(1, slot, 2, C_PASSES)
        store_time(end_strip, 0, SCALAR)
        store_time(end_strip, 1, VECTOR)
        store_unit(1, 2, SCALAR)
        store_unit(1, 3, VECTOR)
